import numpy as np
import ml_dtypes


def mxq(x, axis, fmt="e4m3"):
    dtype, down = {"e4m3": (ml_dtypes.float8_e4m3fn, 7), "e5m2": (ml_dtypes.float8_e5m2, 14)}[fmt]
    v = np.moveaxis(np.asarray(x, np.float32).astype(ml_dtypes.bfloat16).astype(np.float64), axis, -1)
    blocks = v.reshape(v.shape[:-1] + (-1, 32))
    amax = np.abs(blocks).max(-1, keepdims=True)
    byte = np.maximum(np.where(amax > 0, np.frexp(amax)[1] - 1 + 127, 0) - down, 1)
    scale = np.exp2(byte - 127.0)
    codes = (blocks / scale).astype(np.float32).astype(dtype).astype(np.float64)
    return np.moveaxis((codes * scale).reshape(v.shape), -1, axis)


WIDE = False


def mx_kscale(k):
    if not WIDE:
        return np.ones(k)
    levels = np.array([10, -10, 5, -5, 0])
    if k % 512:
        return np.exp2(np.random.permutation(np.resize(levels, k // 32))).repeat(32)
    a = np.empty((k // 512, 16))
    for p in range(k // 512):
        a[p, :8] = np.random.permutation(np.resize(levels, 8))
        for g in range(8):
            far = levels[np.abs(levels - a[p, g]) >= 10]
            a[p, g + 8] = far[np.random.randint(len(far))]
    return np.exp2(a.ravel()).repeat(32)


def f64(x):
    return np.asarray(x).astype(np.float64)


def striped8(idx):
    return np.concatenate([x.reshape(-1, 16).T for x in idx]).astype(np.uint16)


def runs(offs, k):
    lists = np.stack([offs[16 * r : 16 * r + 16].T.reshape(-1) for r in range(8)]).astype(np.int64)
    return lists[np.arange(k) % 512 // 64]


def pack_weight(w):
    k, n = w.shape
    w = f64(np.asarray(w, np.float32).astype(ml_dtypes.bfloat16)).reshape(k // 32, 32, n)
    amax = np.abs(w).max(1)
    byte = np.clip(np.where(amax > 0, np.frexp(amax)[1] - 1 + 127 - 7, 1), 1, 254)
    scaled = (w * np.exp2(127.0 - byte)[:, None, :]).reshape(k, n).astype(np.float32)
    words = np.ascontiguousarray(scaled.reshape(k // 512, 128, 4, n).transpose(0, 1, 3, 2)).astype(ml_dtypes.float8_e4m3fn).view(np.uint8)
    return words, np.ascontiguousarray(byte.astype(np.uint8).reshape(k // 512, 16, n))


def unpack_weight(words, scales):
    g, p, n, _ = words.shape
    vals = np.ascontiguousarray(words).view(ml_dtypes.float8_e4m3fn).astype(np.float64) * np.repeat(np.exp2(scales.astype(np.float64) - 127.0), 8, axis=1)[..., None]
    return vals.transpose(0, 1, 3, 2).reshape(g * 512, n)


def relu(v):
    return np.maximum(v, 0.0)

def planes(y):
    n, m = y.shape
    v = y.astype(np.float32).astype(ml_dtypes.bfloat16).astype(np.float64).reshape(n // 32, 32, m)
    top = np.abs(v).max(1)
    byte = np.clip(np.where(top > 0, np.frexp(top)[1] - 1 + 127 - 7, 1), 1, 254)
    codes = (v * np.exp2(127.0 - byte)[:, None, :]).reshape(n, m).astype(np.float32).astype(ml_dtypes.float8_e4m3fn).view(np.uint8)
    words = codes.reshape(n // 512, 128, 4, m).transpose(0, 1, 3, 2)
    return np.ascontiguousarray(words), np.ascontiguousarray(byte.astype(np.uint8).reshape(n // 512, 16, m))


K, T, S, N = 512, 2048, 512, 512


def setup_inputs():
    n = np.random.standard_normal
    s = mx_kscale(K)[:, None]
    packed_xT = pack_weight(n((K, T)) * s)
    return {
        "x_words": packed_xT[0],
        "x_scales": packed_xT[1],
        "w1": (n((K, N)) / np.sqrt(K) / s).astype(np.float32),
        "w2": (n((K, N)) / np.sqrt(K) / s).astype(np.float32),
        "offs": striped8(np.stack([np.random.permutation(T)[:S] for _ in range(8)])),
        "old": striped8(np.stack([np.random.permutation(T)[:S] for _ in range(8)])),
    }


def reference(x_words, x_scales, w1, w2, offs, old):
    xq = unpack_weight(x_words, x_scales)[np.arange(K)[:, None], runs(offs, K)]
    y = mxq(f64(w1), 0, "e4m3").T @ xq
    xold = unpack_weight(x_words, x_scales)[np.arange(K)[:, None], runs(old, K)]
    e = mxq(f64(w2), 0, "e4m3").T @ xold
    out_0 = relu(y - e)
    return (out_0,) + planes(out_0)

@@ -1,0 +1,136 @@
+from contextlib import ExitStack
+
+import concourse.mybir as mybir
+
+K, T, S, N = 512, 2048, 512, 512
+FLOPS = 2 * 2 * K * N * S
+
+F32 = mybir.dt.float32
+BF16 = mybir.dt.bfloat16
+I32 = mybir.dt.int32
+U32 = mybir.dt.uint32
+U16 = mybir.dt.uint16
+U8 = mybir.dt.uint8
+FP8X4 = mybir.dt.float8_e4m3fn_x4
+COPY = mybir.ActivationFunctionType.Copy
+RELU = mybir.ActivationFunctionType.Relu
+
+P = 128
+PACK = 4
+HALF = S // 2
+
+
+def tile_picked_phdiff_relu_po_kernel(tc, x_words, x_scales, w1, w2, offs, old, out_0, out_1, out_2):
+    nc = tc.nc
+    with ExitStack() as ctx:
+        keep = ctx.enter_context(tc.tile_pool(name="keep", bufs=1))
+        psum = ctx.enter_context(tc.psum_pool(name="psum", bufs=1))
+
+        lists = []
+        for name, src in (("offs", offs), ("old", old)):
+            tile = keep.tile([P, S // 16], U16, name=name + "_list")
+            nc.sync.dma_start(tile[:], src)
+            lists.append(tile)
+
+        scale_table = keep.tile([P, T], U8, align_bytes=64)
+        nc.vector.memset(scale_table[:].bitcast(I32), 0)
+        rows_by_parity = x_scales[0].rearrange("(r e) c -> e r c", e=2)
+        for e in range(2):
+            nc.scalar.dma_start(scale_table[e:P:16, :].bitcast(I32), rows_by_parity[e].bitcast(I32))
+
+        def load_columns(w, name, c0, c1):
+            raw = keep.tile([P, PACK, c1 - c0], F32, name=name)
+            nc.sync.dma_start(raw[:], w.rearrange("(p j) c -> p j c", j=PACK)[:, :, c0:c1])
+            return raw
+
+        w1_raw = load_columns(w1, "w1_raw", 0, N)
+        word_table = keep.tile([P, T], I32, align_bytes=64)
+        nc.sync.dma_start(word_table[:], x_words[0].rearrange("p c r -> p (c r)").bitcast(I32))
+        w2_cuts = (0, 256, 384, 512)
+        w2_raw = [load_columns(w2, "w2_raw%d" % i, w2_cuts[i], w2_cuts[i + 1]) for i in range(3)]
+
+        picked_scales = keep.tile([P, 2 * S], U8, align_bytes=64)
+        for i in range(2):
+            nc.vector.tensor_copy(picked_scales[:, i * S : (i + 1) * S], scale_table[:].indirect(lists[i][:]))
+        x_planes = keep.tile([P, 2 * S], U8, align_bytes=64)
+        nc.vector.tensor_copy(x_planes[:].bitcast(I32), picked_scales[:].bitcast(I32))
+        for e in range(2):
+            nc.scalar.dma_start(x_planes[2 + e : P : 32, :].bitcast(I32), picked_scales[16 + e : P : 32, :].bitcast(I32))
+
+        def round_and_deal(engine, grouped, raw, c0, m0, m1, sign):
+            dst = grouped[:].rearrange("p (t m j) -> p m t j", t=PACK, j=PACK)[:, m0:m1]
+            src = raw[:].rearrange("p j (m t) -> p m t j", t=PACK)[:, m0 - c0 // PACK : m1 - c0 // PACK]
+            if engine is nc.scalar:
+                nc.scalar.activation(dst, src, COPY, scale=sign)
+            else:
+                nc.vector.tensor_scalar_mul(dst, src, sign)
+
+        def quantise(grouped, name):
+            codes = keep.tile([P, N], U32, name=name + "_codes", align_bytes=64)
+            scales = keep.tile([P, N], U8, name=name + "_scales", align_bytes=64)
+            for t in range(PACK):
+                cols = slice(t * P, (t + 1) * P)
+                nc.vector.quantize_mx(out=codes[:, cols].bitcast(FP8X4), scales=scales[:, cols], in_=grouped[:, t * N : (t + 1) * N])
+            return codes, scales
+
+        w1_grouped = keep.tile([P, PACK * N], BF16, align_bytes=64)
+        round_and_deal(nc.scalar, w1_grouped, w1_raw, 0, 0, 64, 1.0)
+        round_and_deal(nc.vector, w1_grouped, w1_raw, 0, 64, 128, 1.0)
+        w1_mx = quantise(w1_grouped, "w1")
+
+        picked_words = []
+        for i in range(2):
+            words = keep.tile([P, S], U32, name="picked_words%d" % i, align_bytes=64)
+            nc.vector.tensor_copy(words[:], word_table[:].bitcast(U32).indirect(lists[i][:]))
+            picked_words.append(words)
+
+        banks = [[psum.tile([P, HALF], F32, name="bank%d_%d" % (h, t)) for t in range(PACK)] for h in range(2)]
+
+        def passes(i, w_mx):
+            codes, scales = w_mx
+            for h in range(2):
+                for t in range(PACK):
+                    cols = slice(t * P, (t + 1) * P)
+                    nc.tensor.matmul_mx(
+                        out=banks[h][t][:],
+                        lhsT=codes[:, cols].bitcast(FP8X4),
+                        lhsT_scale=scales[:, cols],
+                        rhs=picked_words[i][:, h * HALF : (h + 1) * HALF].bitcast(FP8X4),
+                        rhs_scale=x_planes[:, i * S + h * HALF : i * S + (h + 1) * HALF],
+                        start=(i == 0),
+                        stop=(i == 1),
+                    )
+
+        passes(0, w1_mx)
+
+        w2_grouped = keep.tile([P, PACK * N], BF16, align_bytes=64)
+        round_and_deal(nc.scalar, w2_grouped, w2_raw[0], 0, 0, 64, -1.0)
+        round_and_deal(nc.vector, w2_grouped, w2_raw[1], 256, 64, 96, -1.0)
+        round_and_deal(nc.vector, w2_grouped, w2_raw[2], 384, 96, 128, -1.0)
+        w2_mx = quantise(w2_grouped, "w2")
+        passes(1, w2_mx)
+
+        out_rows = out_0.rearrange("(p t) j -> p t j", t=PACK)
+        out_words = out_1[0].rearrange("p c r -> p (c r)").bitcast(I32)
+        y_scales = keep.tile([P, S], U8, align_bytes=64)
+        for h in range(2):
+            cols = slice(h * HALF, (h + 1) * HALF)
+            y = keep.tile([P, PACK, HALF], F32, name="y%d" % h)
+            for t in range(PACK):
+                if h == 0 and t >= 2:
+                    nc.vector.tensor_scalar_max(y[:, t, :], banks[h][t][:], 0.0)
+                else:
+                    nc.scalar.activation(y[:, t, :], banks[h][t][:], RELU)
+                if t % 2 == 1:
+                    nc.sync.dma_start(out_rows[:, t - 1 : t + 1, cols], y[:, t - 1 : t + 1, :])
+            y_grouped = keep.tile([P, HALF * PACK], BF16, name="y_grouped%d" % h, align_bytes=64)
+            nc.vector.tensor_copy(
+                y_grouped[:].rearrange("p (c i t) -> p c t i", i=4, t=PACK),
+                y[:].rearrange("p t (c i) -> p c t i", i=4),
+            )
+            y_codes = keep.tile([P, HALF], U32, name="y_codes%d" % h, align_bytes=64)
+            nc.vector.quantize_mx(out=y_codes[:].bitcast(FP8X4), scales=y_scales[:, cols], in_=y_grouped[:])
+            nc.sync.dma_start(out_words[:, cols], y_codes[:].bitcast(I32))
+        for q in range(4):
+            queue = nc.scalar if q % 2 else nc.sync
+            queue.dma_start(out_2[0][4 * q : 4 * q + 4, :].bitcast(I32), y_scales[32 * q : 32 * q + 4, :].bitcast(I32))

@@ -24,6 +24,7 @@ def tile_picked_phdiff_relu_po_kernel(tc, x_words, x_scales, w1, w2, offs, old, 
     nc = tc.nc
     with ExitStack() as ctx:
         keep = ctx.enter_context(tc.tile_pool(name="keep", bufs=1))
+        stage = ctx.enter_context(tc.tile_pool(name="stage", bufs=1))
         psum = ctx.enter_context(tc.psum_pool(name="psum", bufs=1))
 
         lists = []
@@ -32,34 +33,47 @@ def tile_picked_phdiff_relu_po_kernel(tc, x_words, x_scales, w1, w2, offs, old, 
             nc.sync.dma_start(tile[:], src)
             lists.append(tile)
 
-        scale_table = keep.tile([P, T], U8, align_bytes=64)
+        word_table = keep.tile([P, T], I32, align_bytes=64)
+        x_rows = x_words[0].rearrange("p c r -> p (c r)").bitcast(I32)
+        nc.sync.dma_start(word_table[:, : T // 8], x_rows[:, : T // 8])
+        scale_table = stage.tile([P, T], U8, offset=1024)
         nc.vector.memset(scale_table[:].bitcast(I32), 0)
-        rows_by_parity = x_scales[0].rearrange("(r e) c -> e r c", e=2)
-        for e in range(2):
-            nc.scalar.dma_start(scale_table[e:P:16, :].bitcast(I32), rows_by_parity[e].bitcast(I32))
+        nc.sync.dma_start(scale_table[0:P:8, :].bitcast(I32), x_scales[0].bitcast(I32))
+        x_planes = keep.tile([P, 2 * S], U8, align_bytes=64)
+        nc.vector.memset(x_planes[:].bitcast(I32), 0)
 
-        def load_columns(w, name, c0, c1):
-            raw = keep.tile([P, PACK, c1 - c0], F32, name=name)
+        warm = keep.tile([P, 8], F32)
+        nc.vector.memset(warm[:], 0.0)
+        warmed = keep.tile([P, 8], F32)
+        nc.scalar.activation(warmed[:], warm[:], RELU)
+
+        def load_columns(raw, w, c0):
+            c1 = c0 + raw.shape[2]
             nc.sync.dma_start(raw[:], w.rearrange("(p j) c -> p j c", j=PACK)[:, :, c0:c1])
             return raw
 
-        w1_raw = load_columns(w1, "w1_raw", 0, N)
-        word_table = keep.tile([P, T], I32, align_bytes=64)
-        nc.sync.dma_start(word_table[:], x_words[0].rearrange("p c r -> p (c r)").bitcast(I32))
-        w2_cuts = (0, 256, 384, 512)
-        w2_raw = [load_columns(w2, "w2_raw%d" % i, w2_cuts[i], w2_cuts[i + 1]) for i in range(3)]
+        nc.sync.dma_start(word_table[:, T // 8 :], x_rows[:, T // 8 :])
+        w1_raw = [load_columns(keep.tile([P, PACK, n], F32, name="w1_raw%d" % c0), w1, c0) for c0, n in ((0, 256), (256, 256))]
+        w2_first = load_columns(keep.tile([P, PACK, 256], F32, name="w2_first"), w2, 0)
 
         picked_scales = keep.tile([P, 2 * S], U8, align_bytes=64)
         for i in range(2):
             nc.vector.tensor_copy(picked_scales[:, i * S : (i + 1) * S], scale_table[:].indirect(lists[i][:]))
-        x_planes = keep.tile([P, 2 * S], U8, align_bytes=64)
-        nc.vector.tensor_copy(x_planes[:].bitcast(I32), picked_scales[:].bitcast(I32))
-        for e in range(2):
-            nc.scalar.dma_start(x_planes[2 + e : P : 32, :].bitcast(I32), picked_scales[16 + e : P : 32, :].bitcast(I32))
+        for q in range(4):
+            nc.sync.dma_start(x_planes[32 * q : 32 * q + 4, :].bitcast(I32), picked_scales[32 * q : 32 * q + 32 : 8, :].bitcast(I32))
+        w2_mid = load_columns(stage.tile([P, PACK, 128], F32, name="w2_mid", offset=0), w2, 256)
+        w2_last = load_columns(stage.tile([P, PACK, 128], F32, name="w2_last", offset=2048), w2, 384)
+
+        def gather_words(words, offsets):
+            nc.vector.tensor_copy(words[:], word_table[:].bitcast(U32).indirect(offsets))
+            return words
+
+        now_words = gather_words(keep.tile([P, S], U32, name="now_words", align_bytes=64), lists[0][:])
+        old_low = gather_words(keep.tile([P, HALF], U32, name="old_low", align_bytes=64), lists[1][:, :16])
 
         def round_and_deal(engine, grouped, raw, c0, m0, m1, sign):
-            dst = grouped[:].rearrange("p (t m j) -> p m t j", t=PACK, j=PACK)[:, m0:m1]
-            src = raw[:].rearrange("p j (m t) -> p m t j", t=PACK)[:, m0 - c0 // PACK : m1 - c0 // PACK]
+            dst = grouped[:].rearrange("p (t m j) -> p m j t", t=PACK, j=PACK)[:, m0:m1]
+            src = raw[:].rearrange("p j (m t) -> p m j t", t=PACK)[:, m0 - c0 // PACK : m1 - c0 // PACK]
             if engine is nc.scalar:
                 nc.scalar.activation(dst, src, COPY, scale=sign)
             else:
@@ -73,42 +87,41 @@ def tile_picked_phdiff_relu_po_kernel(tc, x_words, x_scales, w1, w2, offs, old, 
                 nc.vector.quantize_mx(out=codes[:, cols].bitcast(FP8X4), scales=scales[:, cols], in_=grouped[:, t * N : (t + 1) * N])
             return codes, scales
 
-        w1_grouped = keep.tile([P, PACK * N], BF16, align_bytes=64)
-        round_and_deal(nc.scalar, w1_grouped, w1_raw, 0, 0, 64, 1.0)
-        round_and_deal(nc.vector, w1_grouped, w1_raw, 0, 64, 128, 1.0)
+        w1_grouped = keep.tile([P, PACK * N], BF16, tag="reused", align_bytes=64)
+        round_and_deal(nc.scalar, w1_grouped, w1_raw[0], 0, 0, 64, 1.0)
+        round_and_deal(nc.scalar, w1_grouped, w1_raw[1], 256, 64, 86, 1.0)
+        round_and_deal(nc.vector, w1_grouped, w1_raw[1], 256, 86, 128, 1.0)
         w1_mx = quantise(w1_grouped, "w1")
-
-        picked_words = []
-        for i in range(2):
-            words = keep.tile([P, S], U32, name="picked_words%d" % i, align_bytes=64)
-            nc.vector.tensor_copy(words[:], word_table[:].bitcast(U32).indirect(lists[i][:]))
-            picked_words.append(words)
+        old_high = gather_words(keep.tile([P, HALF], U32, name="old_high", tag="reused", align_bytes=64), lists[1][:, 16:])
+        picked_words = [[now_words[:, :HALF], now_words[:, HALF:]], [old_low[:], old_high[:]]]
 
         banks = [[psum.tile([P, HALF], F32, name="bank%d_%d" % (h, t)) for t in range(PACK)] for h in range(2)]
 
-        def passes(i, w_mx):
+        def passes(i, w_mx, halves):
             codes, scales = w_mx
-            for h in range(2):
+            for h in halves:
                 for t in range(PACK):
                     cols = slice(t * P, (t + 1) * P)
                     nc.tensor.matmul_mx(
                         out=banks[h][t][:],
                         lhsT=codes[:, cols].bitcast(FP8X4),
                         lhsT_scale=scales[:, cols],
-                        rhs=picked_words[i][:, h * HALF : (h + 1) * HALF].bitcast(FP8X4),
+                        rhs=picked_words[i][h].bitcast(FP8X4),
                         rhs_scale=x_planes[:, i * S + h * HALF : i * S + (h + 1) * HALF],
                         start=(i == 0),
                         stop=(i == 1),
                     )
 
-        passes(0, w1_mx)
+        passes(0, w1_mx, (0,))
 
         w2_grouped = keep.tile([P, PACK * N], BF16, align_bytes=64)
-        round_and_deal(nc.scalar, w2_grouped, w2_raw[0], 0, 0, 64, -1.0)
-        round_and_deal(nc.vector, w2_grouped, w2_raw[1], 256, 64, 96, -1.0)
-        round_and_deal(nc.vector, w2_grouped, w2_raw[2], 384, 96, 128, -1.0)
+        round_and_deal(nc.scalar, w2_grouped, w2_first, 0, 0, 64, -1.0)
+        round_and_deal(nc.scalar, w2_grouped, w2_mid, 256, 64, 96, -1.0)
+        round_and_deal(nc.vector, w2_grouped, w2_last, 384, 96, 128, -1.0)
         w2_mx = quantise(w2_grouped, "w2")
-        passes(1, w2_mx)
+        passes(1, w2_mx, (0,))
+        passes(0, w1_mx, (1,))
+        passes(1, w2_mx, (1,))
 
         out_rows = out_0.rearrange("(p t) j -> p t j", t=PACK)
         out_words = out_1[0].rearrange("p c r -> p (c r)").bitcast(I32)
@@ -121,15 +134,22 @@ def tile_picked_phdiff_relu_po_kernel(tc, x_words, x_scales, w1, w2, offs, old, 
                     nc.vector.tensor_scalar_max(y[:, t, :], banks[h][t][:], 0.0)
                 else:
                     nc.scalar.activation(y[:, t, :], banks[h][t][:], RELU)
-                if t % 2 == 1:
+                if h == 0 and t < 2:
+                    nc.sync.dma_start(out_rows[:, t, cols], y[:, t, :])
+                elif t % 2 == 1:
                     nc.sync.dma_start(out_rows[:, t - 1 : t + 1, cols], y[:, t - 1 : t + 1, :])
             y_grouped = keep.tile([P, HALF * PACK], BF16, name="y_grouped%d" % h, align_bytes=64)
-            nc.vector.tensor_copy(
-                y_grouped[:].rearrange("p (c i t) -> p c t i", i=4, t=PACK),
-                y[:].rearrange("p t (c i) -> p c t i", i=4),
-            )
+            dst = y_grouped[:].rearrange("p (c i t) -> p c t i", i=4, t=PACK)
+            src = y[:].rearrange("p t (c i) -> p c t i", i=4)
+            if h == 0:
+                nc.vector.tensor_copy(dst, src)
+            else:
+                nc.vector.tensor_copy(dst[:, :32], src[:, :32])
+                nc.scalar.copy(dst[:, 32:], src[:, 32:])
             y_codes = keep.tile([P, HALF], U32, name="y_codes%d" % h, align_bytes=64)
-            nc.vector.quantize_mx(out=y_codes[:].bitcast(FP8X4), scales=y_scales[:, cols], in_=y_grouped[:])
+            pieces = ((0, HALF),) if h == 0 else ((HALF // 2, HALF), (0, HALF // 2))
+            for c0, c1 in pieces:
+                nc.vector.quantize_mx(out=y_codes[:, c0:c1].bitcast(FP8X4), scales=y_scales[:, h * HALF + c0 : h * HALF + c1], in_=y_grouped[:, PACK * c0 : PACK * c1])
             nc.sync.dma_start(out_words[:, cols], y_codes[:].bitcast(I32))
         for q in range(4):
             queue = nc.scalar if q % 2 else nc.sync

@@ -36,7 +36,7 @@ def tile_picked_phdiff_relu_po_kernel(tc, x_words, x_scales, w1, w2, offs, old, 
         word_table = keep.tile([P, T], I32, align_bytes=64)
         x_rows = x_words[0].rearrange("p c r -> p (c r)").bitcast(I32)
         nc.sync.dma_start(word_table[:, : T // 8], x_rows[:, : T // 8])
-        scale_table = stage.tile([P, T], U8, offset=1024)
+        scale_table = stage.tile([P, T], U8, offset=2048)
         nc.vector.memset(scale_table[:].bitcast(I32), 0)
         nc.sync.dma_start(scale_table[0:P:8, :].bitcast(I32), x_scales[0].bitcast(I32))
         x_planes = keep.tile([P, 2 * S], U8, align_bytes=64)
@@ -52,24 +52,22 @@ def tile_picked_phdiff_relu_po_kernel(tc, x_words, x_scales, w1, w2, offs, old, 
             nc.sync.dma_start(raw[:], w.rearrange("(p j) c -> p j c", j=PACK)[:, :, c0:c1])
             return raw
 
-        nc.sync.dma_start(word_table[:, T // 8 :], x_rows[:, T // 8 :])
         w1_raw = [load_columns(keep.tile([P, PACK, n], F32, name="w1_raw%d" % c0), w1, c0) for c0, n in ((0, 256), (256, 256))]
-        w2_first = load_columns(keep.tile([P, PACK, 256], F32, name="w2_first"), w2, 0)
+        nc.sync.dma_start(word_table[:, T // 8 :], x_rows[:, T // 8 :])
+        w2_first = load_columns(keep.tile([P, PACK, 192], F32, name="w2_first"), w2, 0)
 
         picked_scales = keep.tile([P, 2 * S], U8, align_bytes=64)
         for i in range(2):
             nc.vector.tensor_copy(picked_scales[:, i * S : (i + 1) * S], scale_table[:].indirect(lists[i][:]))
         for q in range(4):
             nc.sync.dma_start(x_planes[32 * q : 32 * q + 4, :].bitcast(I32), picked_scales[32 * q : 32 * q + 32 : 8, :].bitcast(I32))
-        w2_mid = load_columns(stage.tile([P, PACK, 128], F32, name="w2_mid", offset=0), w2, 256)
-        w2_last = load_columns(stage.tile([P, PACK, 128], F32, name="w2_last", offset=2048), w2, 384)
+        w2_second = load_columns(stage.tile([P, PACK, 192], F32, name="w2_second", offset=0), w2, 192)
+        w2_last = load_columns(stage.tile([P, PACK, 128], F32, name="w2_last", offset=3072), w2, 384)
 
         def gather_words(words, offsets):
             nc.vector.tensor_copy(words[:], word_table[:].bitcast(U32).indirect(offsets))
             return words
 
-        now_words = gather_words(keep.tile([P, S], U32, name="now_words", align_bytes=64), lists[0][:])
-        old_low = gather_words(keep.tile([P, HALF], U32, name="old_low", align_bytes=64), lists[1][:, :16])
 
         def round_and_deal(engine, grouped, raw, c0, m0, m1, sign):
             dst = grouped[:].rearrange("p (t m j) -> p m j t", t=PACK, j=PACK)[:, m0:m1]
@@ -79,21 +77,23 @@ def tile_picked_phdiff_relu_po_kernel(tc, x_words, x_scales, w1, w2, offs, old, 
             else:
                 nc.vector.tensor_scalar_mul(dst, src, sign)
 
-        def quantise(grouped, name):
+        def quantise(grouped, name, step):
             codes = keep.tile([P, N], U32, name=name + "_codes", align_bytes=64)
             scales = keep.tile([P, N], U8, name=name + "_scales", align_bytes=64)
-            for t in range(PACK):
-                cols = slice(t * P, (t + 1) * P)
-                nc.vector.quantize_mx(out=codes[:, cols].bitcast(FP8X4), scales=scales[:, cols], in_=grouped[:, t * N : (t + 1) * N])
+            for t in range(0, PACK, step):
+                cols = slice(t * P, (t + step) * P)
+                nc.vector.quantize_mx(out=codes[:, cols].bitcast(FP8X4), scales=scales[:, cols], in_=grouped[:, t * N : (t + step) * N])
             return codes, scales
 
-        w1_grouped = keep.tile([P, PACK * N], BF16, tag="reused", align_bytes=64)
+        w1_grouped = keep.tile([P, PACK * N], BF16, align_bytes=64)
         round_and_deal(nc.scalar, w1_grouped, w1_raw[0], 0, 0, 64, 1.0)
-        round_and_deal(nc.scalar, w1_grouped, w1_raw[1], 256, 64, 86, 1.0)
-        round_and_deal(nc.vector, w1_grouped, w1_raw[1], 256, 86, 128, 1.0)
-        w1_mx = quantise(w1_grouped, "w1")
-        old_high = gather_words(keep.tile([P, HALF], U32, name="old_high", tag="reused", align_bytes=64), lists[1][:, 16:])
-        picked_words = [[now_words[:, :HALF], now_words[:, HALF:]], [old_low[:], old_high[:]]]
+        round_and_deal(nc.scalar, w1_grouped, w1_raw[1], 256, 64, 104, 1.0)
+        round_and_deal(nc.vector, w1_grouped, w1_raw[1], 256, 104, 128, 1.0)
+        w1_mx = quantise(w1_grouped, "w1", PACK)
+        picked_words = [
+            [gather_words(keep.tile([P, HALF], U32, name="words%d_%d" % (i, h), align_bytes=64), lists[i][:, 16 * h : 16 * h + 16])[:] for h in range(2)]
+            for i in range(2)
+        ]
 
         banks = [[psum.tile([P, HALF], F32, name="bank%d_%d" % (h, t)) for t in range(PACK)] for h in range(2)]
 
@@ -112,25 +112,26 @@ def tile_picked_phdiff_relu_po_kernel(tc, x_words, x_scales, w1, w2, offs, old, 
                         stop=(i == 1),
                     )
 
-        passes(0, w1_mx, (0,))
+        passes(0, w1_mx, (0, 1))
 
         w2_grouped = keep.tile([P, PACK * N], BF16, align_bytes=64)
-        round_and_deal(nc.scalar, w2_grouped, w2_first, 0, 0, 64, -1.0)
-        round_and_deal(nc.scalar, w2_grouped, w2_mid, 256, 64, 96, -1.0)
-        round_and_deal(nc.vector, w2_grouped, w2_last, 384, 96, 128, -1.0)
-        w2_mx = quantise(w2_grouped, "w2")
-        passes(1, w2_mx, (0,))
-        passes(0, w1_mx, (1,))
-        passes(1, w2_mx, (1,))
+        round_and_deal(nc.scalar, w2_grouped, w2_first, 0, 0, 48, -1.0)
+        round_and_deal(nc.scalar, w2_grouped, w2_second, 192, 48, 84, -1.0)
+        round_and_deal(nc.vector, w2_grouped, w2_second, 192, 84, 96, -1.0)
+        round_and_deal(nc.scalar, w2_grouped, w2_last, 384, 96, 104, -1.0)
+        round_and_deal(nc.vector, w2_grouped, w2_last, 384, 104, 128, -1.0)
+        w2_mx = quantise(w2_grouped, "w2", 1)
+        passes(1, w2_mx, (0, 1))
 
         out_rows = out_0.rearrange("(p t) j -> p t j", t=PACK)
         out_words = out_1[0].rearrange("p c r -> p (c r)").bitcast(I32)
         y_scales = keep.tile([P, S], U8, align_bytes=64)
+        codes_out = []
         for h in range(2):
             cols = slice(h * HALF, (h + 1) * HALF)
             y = keep.tile([P, PACK, HALF], F32, name="y%d" % h)
             for t in range(PACK):
-                if h == 0 and t >= 2:
+                if h == 0 and t % 2 == 1:
                     nc.vector.tensor_scalar_max(y[:, t, :], banks[h][t][:], 0.0)
                 else:
                     nc.scalar.activation(y[:, t, :], banks[h][t][:], RELU)
@@ -141,15 +142,17 @@ def tile_picked_phdiff_relu_po_kernel(tc, x_words, x_scales, w1, w2, offs, old, 
             y_grouped = keep.tile([P, HALF * PACK], BF16, name="y_grouped%d" % h, align_bytes=64)
             dst = y_grouped[:].rearrange("p (c i t) -> p c t i", i=4, t=PACK)
             src = y[:].rearrange("p t (c i) -> p c t i", i=4)
+            nc.vector.tensor_copy(dst[:, :32], src[:, :32])
             if h == 0:
-                nc.vector.tensor_copy(dst, src)
+                nc.vector.tensor_copy(dst[:, 32:], src[:, 32:])
             else:
-                nc.vector.tensor_copy(dst[:, :32], src[:, :32])
-                nc.scalar.copy(dst[:, 32:], src[:, 32:])
+                nc.vector.tensor_copy(dst[:, 32:44], src[:, 32:44])
+                nc.scalar.copy(dst[:, 44:], src[:, 44:])
             y_codes = keep.tile([P, HALF], U32, name="y_codes%d" % h, align_bytes=64)
-            pieces = ((0, HALF),) if h == 0 else ((HALF // 2, HALF), (0, HALF // 2))
-            for c0, c1 in pieces:
+            for c0, c1 in ((0, HALF // 2), (HALF // 2, HALF)):
                 nc.vector.quantize_mx(out=y_codes[:, c0:c1].bitcast(FP8X4), scales=y_scales[:, h * HALF + c0 : h * HALF + c1], in_=y_grouped[:, PACK * c0 : PACK * c1])
+            codes_out.append((cols, y_codes))
+        for cols, y_codes in codes_out:
             nc.sync.dma_start(out_words[:, cols], y_codes[:].bitcast(I32))
         for q in range(4):
             queue = nc.scalar if q % 2 else nc.sync

@@ -27,42 +27,45 @@ def tile_picked_phdiff_relu_po_kernel(tc, x_words, x_scales, w1, w2, offs, old, 
         stage = ctx.enter_context(tc.tile_pool(name="stage", bufs=1))
         psum = ctx.enter_context(tc.psum_pool(name="psum", bufs=1))
 
+        def load_columns(raw, w, c0):
+            c1 = c0 + raw.shape[2]
+            nc.sync.dma_start(raw[:], w.rearrange("(p j) c -> p j c", j=PACK)[:, :, c0:c1])
+            return raw
+
+        w1_first = load_columns(keep.tile([P, PACK, 128], F32, name="w1_first"), w1, 0)
         lists = []
         for name, src in (("offs", offs), ("old", old)):
             tile = keep.tile([P, S // 16], U16, name=name + "_list")
             nc.sync.dma_start(tile[:], src)
             lists.append(tile)
 
-        word_table = keep.tile([P, T], I32, align_bytes=64)
-        x_rows = x_words[0].rearrange("p c r -> p (c r)").bitcast(I32)
-        nc.sync.dma_start(word_table[:, : T // 8], x_rows[:, : T // 8])
-        scale_table = stage.tile([P, T], U8, offset=2048)
+        scale_table = keep.tile([P, T], U8)
         nc.vector.memset(scale_table[:].bitcast(I32), 0)
         nc.sync.dma_start(scale_table[0:P:8, :].bitcast(I32), x_scales[0].bitcast(I32))
-        x_planes = keep.tile([P, 2 * S], U8, align_bytes=64)
-        nc.vector.memset(x_planes[:].bitcast(I32), 0)
+        now_plane = keep.tile([P, S], U8, align_bytes=64)
+        nc.vector.memset(now_plane[:].bitcast(I32), 0)
 
         warm = keep.tile([P, 8], F32)
         nc.vector.memset(warm[:], 0.0)
         warmed = keep.tile([P, 8], F32)
         nc.scalar.activation(warmed[:], warm[:], RELU)
 
-        def load_columns(raw, w, c0):
-            c1 = c0 + raw.shape[2]
-            nc.sync.dma_start(raw[:], w.rearrange("(p j) c -> p j c", j=PACK)[:, :, c0:c1])
-            return raw
+        w1_second = load_columns(stage.tile([P, PACK, 192], F32, name="w1_second", offset=0), w1, 128)
+        w1_last = load_columns(stage.tile([P, PACK, 192], F32, name="w1_last", offset=5120), w1, 320)
+        word_table = keep.tile([P, T], I32, align_bytes=64)
+        nc.sync.dma_start(word_table[:], x_words[0].rearrange("p c r -> p (c r)").bitcast(I32))
 
-        w1_raw = [load_columns(keep.tile([P, PACK, n], F32, name="w1_raw%d" % c0), w1, c0) for c0, n in ((0, 256), (256, 256))]
-        nc.sync.dma_start(word_table[:, T // 8 :], x_rows[:, T // 8 :])
-        w2_first = load_columns(keep.tile([P, PACK, 192], F32, name="w2_first"), w2, 0)
-
-        picked_scales = keep.tile([P, 2 * S], U8, align_bytes=64)
+        picked_scales = []
         for i in range(2):
-            nc.vector.tensor_copy(picked_scales[:, i * S : (i + 1) * S], scale_table[:].indirect(lists[i][:]))
-        for q in range(4):
-            nc.sync.dma_start(x_planes[32 * q : 32 * q + 4, :].bitcast(I32), picked_scales[32 * q : 32 * q + 32 : 8, :].bitcast(I32))
-        w2_second = load_columns(stage.tile([P, PACK, 192], F32, name="w2_second", offset=0), w2, 192)
-        w2_last = load_columns(stage.tile([P, PACK, 128], F32, name="w2_last", offset=3072), w2, 384)
+            picked = keep.tile([P, S], U8, name="picked%d" % i, align_bytes=64)
+            nc.vector.tensor_copy(picked[:], scale_table[:].indirect(lists[i][:]))
+            picked_scales.append(picked)
+
+        def place_scale_rows(plane, picked):
+            for q in range(4):
+                nc.sync.dma_start(plane[32 * q : 32 * q + 4, :].bitcast(I32), picked[32 * q : 32 * q + 32 : 8, :].bitcast(I32))
+
+        place_scale_rows(now_plane, picked_scales[0])
 
         def gather_words(words, offsets):
             nc.vector.tensor_copy(words[:], word_table[:].bitcast(U32).indirect(offsets))
@@ -86,9 +89,16 @@ def tile_picked_phdiff_relu_po_kernel(tc, x_words, x_scales, w1, w2, offs, old, 
             return codes, scales
 
         w1_grouped = keep.tile([P, PACK * N], BF16, align_bytes=64)
-        round_and_deal(nc.scalar, w1_grouped, w1_raw[0], 0, 0, 64, 1.0)
-        round_and_deal(nc.scalar, w1_grouped, w1_raw[1], 256, 64, 104, 1.0)
-        round_and_deal(nc.vector, w1_grouped, w1_raw[1], 256, 104, 128, 1.0)
+        round_and_deal(nc.scalar, w1_grouped, w1_first, 0, 0, 32, 1.0)
+        round_and_deal(nc.scalar, w1_grouped, w1_second, 128, 32, 80, 1.0)
+        round_and_deal(nc.scalar, w1_grouped, w1_last, 320, 80, 128, 1.0)
+        w2_first = load_columns(stage.tile([P, PACK, 192], F32, name="w2_first", offset=0), w2, 0)
+        w2_second = load_columns(stage.tile([P, PACK, 192], F32, name="w2_second", offset=3072), w2, 192)
+        w2_last = load_columns(stage.tile([P, PACK, 128], F32, name="w2_last", offset=6656), w2, 384)
+        old_plane = stage.tile([P, S], U8, offset=6144, align_bytes=64)
+        nc.vector.memset(old_plane[:].bitcast(I32), 0)
+        place_scale_rows(old_plane, picked_scales[1])
+        planes = [now_plane, old_plane]
         w1_mx = quantise(w1_grouped, "w1", PACK)
         picked_words = [
             [gather_words(keep.tile([P, HALF], U32, name="words%d_%d" % (i, h), align_bytes=64), lists[i][:, 16 * h : 16 * h + 16])[:] for h in range(2)]
@@ -107,7 +117,7 @@ def tile_picked_phdiff_relu_po_kernel(tc, x_words, x_scales, w1, w2, offs, old, 
                         lhsT=codes[:, cols].bitcast(FP8X4),
                         lhsT_scale=scales[:, cols],
                         rhs=picked_words[i][h].bitcast(FP8X4),
-                        rhs_scale=x_planes[:, i * S + h * HALF : i * S + (h + 1) * HALF],
+                        rhs_scale=planes[i][:, h * HALF : (h + 1) * HALF],
                         start=(i == 0),
                         stop=(i == 1),
                     )
@@ -126,34 +136,42 @@ def tile_picked_phdiff_relu_po_kernel(tc, x_words, x_scales, w1, w2, offs, old, 
         out_rows = out_0.rearrange("(p t) j -> p t j", t=PACK)
         out_words = out_1[0].rearrange("p c r -> p (c r)").bitcast(I32)
         y_scales = keep.tile([P, S], U8, align_bytes=64)
-        codes_out = []
+        y = [keep.tile([P, PACK, HALF], F32, name="y%d" % h) for h in range(2)]
+        y_grouped = [keep.tile([P, HALF * PACK], BF16, name="y_grouped%d" % h, align_bytes=64) for h in range(2)]
+        y_codes = [keep.tile([P, HALF], U32, name="y_codes%d" % h, align_bytes=64) for h in range(2)]
+        stores = {(0, 0): 0, (0, 1): 1, (0, 3): 2, (1, 1): 0, (1, 3): 2}
         for h in range(2):
-            cols = slice(h * HALF, (h + 1) * HALF)
-            y = keep.tile([P, PACK, HALF], F32, name="y%d" % h)
             for t in range(PACK):
-                if h == 0 and t % 2 == 1:
-                    nc.vector.tensor_scalar_max(y[:, t, :], banks[h][t][:], 0.0)
+                if (h, t) in ((0, 1), (0, 3), (1, 0)):
+                    nc.vector.tensor_scalar_max(y[h][:, t, :], banks[h][t][:], 0.0)
                 else:
-                    nc.scalar.activation(y[:, t, :], banks[h][t][:], RELU)
-                if h == 0 and t < 2:
-                    nc.sync.dma_start(out_rows[:, t, cols], y[:, t, :])
-                elif t % 2 == 1:
-                    nc.sync.dma_start(out_rows[:, t - 1 : t + 1, cols], y[:, t - 1 : t + 1, :])
-            y_grouped = keep.tile([P, HALF * PACK], BF16, name="y_grouped%d" % h, align_bytes=64)
-            dst = y_grouped[:].rearrange("p (c i t) -> p c t i", i=4, t=PACK)
-            src = y[:].rearrange("p t (c i) -> p c t i", i=4)
-            nc.vector.tensor_copy(dst[:, :32], src[:, :32])
-            if h == 0:
-                nc.vector.tensor_copy(dst[:, 32:], src[:, 32:])
+                    nc.scalar.activation(y[h][:, t, :], banks[h][t][:], RELU)
+                if (h, t) in stores:
+                    t0 = stores[(h, t)]
+                    nc.sync.dma_start(out_rows[:, t0 : t + 1, h * HALF : (h + 1) * HALF], y[h][:, t0 : t + 1, :])
+
+        def interleave(engine, h, u):
+            dst = y_grouped[h][:].rearrange("p (c i t) -> p c t i", i=4, t=PACK)[:, 32 * u : 32 * u + 32]
+            src = y[h][:].rearrange("p t (c i) -> p c t i", i=4)[:, 32 * u : 32 * u + 32]
+            if engine is nc.scalar:
+                nc.scalar.copy(dst, src)
             else:
-                nc.vector.tensor_copy(dst[:, 32:44], src[:, 32:44])
-                nc.scalar.copy(dst[:, 44:], src[:, 44:])
-            y_codes = keep.tile([P, HALF], U32, name="y_codes%d" % h, align_bytes=64)
-            for c0, c1 in ((0, HALF // 2), (HALF // 2, HALF)):
-                nc.vector.quantize_mx(out=y_codes[:, c0:c1].bitcast(FP8X4), scales=y_scales[:, h * HALF + c0 : h * HALF + c1], in_=y_grouped[:, PACK * c0 : PACK * c1])
-            codes_out.append((cols, y_codes))
-        for cols, y_codes in codes_out:
-            nc.sync.dma_start(out_words[:, cols], y_codes[:].bitcast(I32))
+                nc.vector.tensor_copy(dst, src)
+
+        def quantise_result(h, u):
+            c0, c1 = u * P, (u + 1) * P
+            nc.vector.quantize_mx(out=y_codes[h][:, c0:c1].bitcast(FP8X4), scales=y_scales[:, h * HALF + c0 : h * HALF + c1], in_=y_grouped[h][:, PACK * c0 : PACK * c1])
+
+        interleave(nc.vector, 0, 0)
+        interleave(nc.vector, 0, 1)
+        quantise_result(0, 0)
+        interleave(nc.vector, 1, 0)
+        interleave(nc.scalar, 1, 1)
+        quantise_result(0, 1)
+        quantise_result(1, 1)
+        quantise_result(1, 0)
+        for h in range(2):
+            nc.sync.dma_start(out_words[:, h * HALF : (h + 1) * HALF], y_codes[h][:].bitcast(I32))
         for q in range(4):
             queue = nc.scalar if q % 2 else nc.sync
             queue.dma_start(out_2[0][4 * q : 4 * q + 4, :].bitcast(I32), y_scales[32 * q : 32 * q + 4, :].bitcast(I32))

@@ -50,8 +50,8 @@ def tile_picked_phdiff_relu_po_kernel(tc, x_words, x_scales, w1, w2, offs, old, 
         warmed = keep.tile([P, 8], F32)
         nc.scalar.activation(warmed[:], warm[:], RELU)
 
-        w1_second = load_columns(stage.tile([P, PACK, 192], F32, name="w1_second", offset=0), w1, 128)
-        w1_last = load_columns(stage.tile([P, PACK, 192], F32, name="w1_last", offset=5120), w1, 320)
+        w1_second = load_columns(stage.tile([P, PACK, 128], F32, name="w1_second", offset=1024), w1, 128)
+        w1_last = load_columns(stage.tile([P, PACK, 256], F32, name="w1_last", offset=6144), w1, 256)
         word_table = keep.tile([P, T], I32, align_bytes=64)
         nc.sync.dma_start(word_table[:], x_words[0].rearrange("p c r -> p (c r)").bitcast(I32))
 
@@ -90,12 +90,13 @@ def tile_picked_phdiff_relu_po_kernel(tc, x_words, x_scales, w1, w2, offs, old, 
 
         w1_grouped = keep.tile([P, PACK * N], BF16, align_bytes=64)
         round_and_deal(nc.scalar, w1_grouped, w1_first, 0, 0, 32, 1.0)
-        round_and_deal(nc.scalar, w1_grouped, w1_second, 128, 32, 80, 1.0)
-        round_and_deal(nc.scalar, w1_grouped, w1_last, 320, 80, 128, 1.0)
-        w2_first = load_columns(stage.tile([P, PACK, 192], F32, name="w2_first", offset=0), w2, 0)
-        w2_second = load_columns(stage.tile([P, PACK, 192], F32, name="w2_second", offset=3072), w2, 192)
-        w2_last = load_columns(stage.tile([P, PACK, 128], F32, name="w2_last", offset=6656), w2, 384)
-        old_plane = stage.tile([P, S], U8, offset=6144, align_bytes=64)
+        round_and_deal(nc.scalar, w1_grouped, w1_second, 128, 32, 64, 1.0)
+        round_and_deal(nc.scalar, w1_grouped, w1_last, 256, 64, 104, 1.0)
+        round_and_deal(nc.vector, w1_grouped, w1_last, 256, 104, 128, 1.0)
+        w2_first = load_columns(stage.tile([P, PACK, 128], F32, name="w2_first", offset=0), w2, 0)
+        w2_second = load_columns(stage.tile([P, PACK, 256], F32, name="w2_second", offset=2048), w2, 128)
+        w2_last = load_columns(stage.tile([P, PACK, 128], F32, name="w2_last", offset=6144), w2, 384)
+        old_plane = stage.tile([P, S], U8, offset=8192, align_bytes=64)
         nc.vector.memset(old_plane[:].bitcast(I32), 0)
         place_scale_rows(old_plane, picked_scales[1])
         planes = [now_plane, old_plane]
@@ -125,9 +126,9 @@ def tile_picked_phdiff_relu_po_kernel(tc, x_words, x_scales, w1, w2, offs, old, 
         passes(0, w1_mx, (0, 1))
 
         w2_grouped = keep.tile([P, PACK * N], BF16, align_bytes=64)
-        round_and_deal(nc.scalar, w2_grouped, w2_first, 0, 0, 48, -1.0)
-        round_and_deal(nc.scalar, w2_grouped, w2_second, 192, 48, 84, -1.0)
-        round_and_deal(nc.vector, w2_grouped, w2_second, 192, 84, 96, -1.0)
+        round_and_deal(nc.scalar, w2_grouped, w2_first, 0, 0, 32, -1.0)
+        round_and_deal(nc.scalar, w2_grouped, w2_second, 128, 32, 72, -1.0)
+        round_and_deal(nc.vector, w2_grouped, w2_second, 128, 72, 96, -1.0)
         round_and_deal(nc.scalar, w2_grouped, w2_last, 384, 96, 104, -1.0)
         round_and_deal(nc.vector, w2_grouped, w2_last, 384, 104, 128, -1.0)
         w2_mx = quantise(w2_grouped, "w2", 1)

@@ -27,33 +27,30 @@ def tile_picked_phdiff_relu_po_kernel(tc, x_words, x_scales, w1, w2, offs, old, 
         stage = ctx.enter_context(tc.tile_pool(name="stage", bufs=1))
         psum = ctx.enter_context(tc.psum_pool(name="psum", bufs=1))
 
-        def load_columns(raw, w, c0):
-            c1 = c0 + raw.shape[2]
-            nc.sync.dma_start(raw[:], w.rearrange("(p j) c -> p j c", j=PACK)[:, :, c0:c1])
-            return raw
-
-        w1_first = load_columns(keep.tile([P, PACK, 128], F32, name="w1_first"), w1, 0)
+        word_table = keep.tile([P, T], I32, align_bytes=64)
+        x_rows = x_words[0].rearrange("p c r -> p (c r)").bitcast(I32)
+        nc.sync.dma_start(word_table[:, : T // 8], x_rows[:, : T // 8])
         lists = []
         for name, src in (("offs", offs), ("old", old)):
             tile = keep.tile([P, S // 16], U16, name=name + "_list")
             nc.sync.dma_start(tile[:], src)
             lists.append(tile)
 
-        scale_table = keep.tile([P, T], U8)
+        scale_table = stage.tile([P, T], U8, offset=0)
         nc.vector.memset(scale_table[:].bitcast(I32), 0)
         nc.sync.dma_start(scale_table[0:P:8, :].bitcast(I32), x_scales[0].bitcast(I32))
-        now_plane = keep.tile([P, S], U8, align_bytes=64)
-        nc.vector.memset(now_plane[:].bitcast(I32), 0)
+        planes = [keep.tile([P, S], U8, name="plane%d" % i, align_bytes=64) for i in range(2)]
+        for plane in planes:
+            nc.vector.memset(plane[:].bitcast(I32), 0)
 
         warm = keep.tile([P, 8], F32)
         nc.vector.memset(warm[:], 0.0)
         warmed = keep.tile([P, 8], F32)
         nc.scalar.activation(warmed[:], warm[:], RELU)
 
-        w1_second = load_columns(stage.tile([P, PACK, 128], F32, name="w1_second", offset=1024), w1, 128)
-        w1_last = load_columns(stage.tile([P, PACK, 256], F32, name="w1_last", offset=6144), w1, 256)
-        word_table = keep.tile([P, T], I32, align_bytes=64)
-        nc.sync.dma_start(word_table[:], x_words[0].rearrange("p c r -> p (c r)").bitcast(I32))
+        w1_raw = keep.tile([P, PACK, N], F32)
+        nc.sync.dma_start(w1_raw[:], w1.rearrange("(p j) c -> p j c", j=PACK))
+        nc.sync.dma_start(word_table[:, T // 8 :], x_rows[:, T // 8 :])
 
         picked_scales = []
         for i in range(2):
@@ -61,26 +58,34 @@ def tile_picked_phdiff_relu_po_kernel(tc, x_words, x_scales, w1, w2, offs, old, 
             nc.vector.tensor_copy(picked[:], scale_table[:].indirect(lists[i][:]))
             picked_scales.append(picked)
 
-        def place_scale_rows(plane, picked):
-            for q in range(4):
-                nc.sync.dma_start(plane[32 * q : 32 * q + 4, :].bitcast(I32), picked[32 * q : 32 * q + 32 : 8, :].bitcast(I32))
+        def place_scale_rows(i):
+            for r in range(4):
+                nc.sync.dma_start(planes[i][r:P:32, :].bitcast(I32), picked_scales[i][8 * r : P : 32, :].bitcast(I32))
 
-        place_scale_rows(now_plane, picked_scales[0])
+        place_scale_rows(0)
+        w2_raw = stage.tile([P, PACK, N], F32, offset=0)
+        nc.sync.dma_start(w2_raw[:], w2.rearrange("(p j) c -> p j c", j=PACK))
+        place_scale_rows(1)
 
         def gather_words(words, offsets):
             nc.vector.tensor_copy(words[:], word_table[:].bitcast(U32).indirect(offsets))
             return words
 
 
-        def round_and_deal(engine, grouped, raw, c0, m0, m1, sign):
-            dst = grouped[:].rearrange("p (t m j) -> p m j t", t=PACK, j=PACK)[:, m0:m1]
-            src = raw[:].rearrange("p j (m t) -> p m j t", t=PACK)[:, m0 - c0 // PACK : m1 - c0 // PACK]
+        def round_and_deal(engine, grouped, raw, u, m0, m1, sign):
+            dst = grouped[:].rearrange("p (t m j) -> p m j t", t=PACK, j=PACK)[:, m0:m1, :, 2 * u : 2 * u + 2]
+            src = raw[:].rearrange("p j (m t) -> p m j t", t=PACK)[:, m0:m1, :, 2 * u : 2 * u + 2]
             if engine is nc.scalar:
                 nc.scalar.activation(dst, src, COPY, scale=sign)
             else:
                 nc.vector.tensor_scalar_mul(dst, src, sign)
 
-        def quantise(grouped, name, step):
+        def quantise(raw, name, sign, step):
+            grouped = keep.tile([P, PACK * N], BF16, name=name + "_grouped", align_bytes=64)
+            round_and_deal(nc.scalar, grouped, raw, 0, 0, 40, sign)
+            round_and_deal(nc.vector, grouped, raw, 0, 40, P, sign)
+            round_and_deal(nc.scalar, grouped, raw, 1, 0, 80, sign)
+            round_and_deal(nc.vector, grouped, raw, 1, 80, P, sign)
             codes = keep.tile([P, N], U32, name=name + "_codes", align_bytes=64)
             scales = keep.tile([P, N], U8, name=name + "_scales", align_bytes=64)
             for t in range(0, PACK, step):
@@ -88,19 +93,7 @@ def tile_picked_phdiff_relu_po_kernel(tc, x_words, x_scales, w1, w2, offs, old, 
                 nc.vector.quantize_mx(out=codes[:, cols].bitcast(FP8X4), scales=scales[:, cols], in_=grouped[:, t * N : (t + step) * N])
             return codes, scales
 
-        w1_grouped = keep.tile([P, PACK * N], BF16, align_bytes=64)
-        round_and_deal(nc.scalar, w1_grouped, w1_first, 0, 0, 32, 1.0)
-        round_and_deal(nc.scalar, w1_grouped, w1_second, 128, 32, 64, 1.0)
-        round_and_deal(nc.scalar, w1_grouped, w1_last, 256, 64, 104, 1.0)
-        round_and_deal(nc.vector, w1_grouped, w1_last, 256, 104, 128, 1.0)
-        w2_first = load_columns(stage.tile([P, PACK, 128], F32, name="w2_first", offset=0), w2, 0)
-        w2_second = load_columns(stage.tile([P, PACK, 256], F32, name="w2_second", offset=2048), w2, 128)
-        w2_last = load_columns(stage.tile([P, PACK, 128], F32, name="w2_last", offset=6144), w2, 384)
-        old_plane = stage.tile([P, S], U8, offset=8192, align_bytes=64)
-        nc.vector.memset(old_plane[:].bitcast(I32), 0)
-        place_scale_rows(old_plane, picked_scales[1])
-        planes = [now_plane, old_plane]
-        w1_mx = quantise(w1_grouped, "w1", PACK)
+        w1_mx = quantise(w1_raw, "w1", 1.0, 2)
         picked_words = [
             [gather_words(keep.tile([P, HALF], U32, name="words%d_%d" % (i, h), align_bytes=64), lists[i][:, 16 * h : 16 * h + 16])[:] for h in range(2)]
             for i in range(2)
@@ -108,71 +101,70 @@ def tile_picked_phdiff_relu_po_kernel(tc, x_words, x_scales, w1, w2, offs, old, 
 
         banks = [[psum.tile([P, HALF], F32, name="bank%d_%d" % (h, t)) for t in range(PACK)] for h in range(2)]
 
-        def passes(i, w_mx, halves):
+        def one_pass(i, w_mx, h, t):
             codes, scales = w_mx
-            for h in halves:
-                for t in range(PACK):
-                    cols = slice(t * P, (t + 1) * P)
-                    nc.tensor.matmul_mx(
-                        out=banks[h][t][:],
-                        lhsT=codes[:, cols].bitcast(FP8X4),
-                        lhsT_scale=scales[:, cols],
-                        rhs=picked_words[i][h].bitcast(FP8X4),
-                        rhs_scale=planes[i][:, h * HALF : (h + 1) * HALF],
-                        start=(i == 0),
-                        stop=(i == 1),
-                    )
+            cols = slice(t * P, (t + 1) * P)
+            nc.tensor.matmul_mx(
+                out=banks[h][t][:],
+                lhsT=codes[:, cols].bitcast(FP8X4),
+                lhsT_scale=scales[:, cols],
+                rhs=picked_words[i][h].bitcast(FP8X4),
+                rhs_scale=planes[i][:, h * HALF : (h + 1) * HALF],
+                start=(i == 0),
+                stop=(i == 1),
+            )
 
-        passes(0, w1_mx, (0, 1))
-
-        w2_grouped = keep.tile([P, PACK * N], BF16, align_bytes=64)
-        round_and_deal(nc.scalar, w2_grouped, w2_first, 0, 0, 32, -1.0)
-        round_and_deal(nc.scalar, w2_grouped, w2_second, 128, 32, 72, -1.0)
-        round_and_deal(nc.vector, w2_grouped, w2_second, 128, 72, 96, -1.0)
-        round_and_deal(nc.scalar, w2_grouped, w2_last, 384, 96, 104, -1.0)
-        round_and_deal(nc.vector, w2_grouped, w2_last, 384, 104, 128, -1.0)
-        w2_mx = quantise(w2_grouped, "w2", 1)
-        passes(1, w2_mx, (0, 1))
+        for h in range(2):
+            for t in range(PACK):
+                one_pass(0, w1_mx, h, t)
+        w2_mx = quantise(w2_raw, "w2", -1.0, 1)
+        for t in range(PACK):
+            for h in range(2):
+                one_pass(1, w2_mx, h, t)
 
         out_rows = out_0.rearrange("(p t) j -> p t j", t=PACK)
         out_words = out_1[0].rearrange("p c r -> p (c r)").bitcast(I32)
         y_scales = keep.tile([P, S], U8, align_bytes=64)
-        y = [keep.tile([P, PACK, HALF], F32, name="y%d" % h) for h in range(2)]
-        y_grouped = [keep.tile([P, HALF * PACK], BF16, name="y_grouped%d" % h, align_bytes=64) for h in range(2)]
-        y_codes = [keep.tile([P, HALF], U32, name="y_codes%d" % h, align_bytes=64) for h in range(2)]
-        stores = {(0, 0): 0, (0, 1): 1, (0, 3): 2, (1, 1): 0, (1, 3): 2}
-        for h in range(2):
-            for t in range(PACK):
-                if (h, t) in ((0, 1), (0, 3), (1, 0)):
-                    nc.vector.tensor_scalar_max(y[h][:, t, :], banks[h][t][:], 0.0)
+        y = keep.tile([P, PACK, S], F32)
+        for t in range(PACK):
+            for h in range(2):
+                cols = slice(h * HALF, (h + 1) * HALF)
+                if (t, h) in ((1, 0), (1, 1), (2, 1)):
+                    nc.vector.tensor_scalar_max(y[:, t, cols], banks[h][t][:], 0.0)
                 else:
-                    nc.scalar.activation(y[h][:, t, :], banks[h][t][:], RELU)
-                if (h, t) in stores:
-                    t0 = stores[(h, t)]
-                    nc.sync.dma_start(out_rows[:, t0 : t + 1, h * HALF : (h + 1) * HALF], y[h][:, t0 : t + 1, :])
+                    nc.scalar.activation(y[:, t, cols], banks[h][t][:], RELU)
+                if t == 0:
+                    nc.sync.dma_start(out_rows[:, t, cols], y[:, t, cols])
+            if t == 1:
+                nc.sync.dma_start(out_rows[:, t, :], y[:, t, :])
+        nc.sync.dma_start(out_rows[:, 2:, :], y[:, 2:, :])
 
-        def interleave(engine, h, u):
-            dst = y_grouped[h][:].rearrange("p (c i t) -> p c t i", i=4, t=PACK)[:, 32 * u : 32 * u + 32]
-            src = y[h][:].rearrange("p t (c i) -> p c t i", i=4)[:, 32 * u : 32 * u + 32]
+        y_grouped = keep.tile([P, S * PACK], BF16, align_bytes=64)
+        y_codes = keep.tile([P, S], U32, align_bytes=64)
+
+        def interleave(engine, c0, c1):
+            dst = y_grouped[:].rearrange("p (c i t) -> p c t i", i=4, t=PACK)[:, c0 // 4 : c1 // 4]
+            src = y[:].rearrange("p t (c i) -> p c t i", i=4)[:, c0 // 4 : c1 // 4]
             if engine is nc.scalar:
                 nc.scalar.copy(dst, src)
             else:
                 nc.vector.tensor_copy(dst, src)
 
-        def quantise_result(h, u):
+        def quantise_result(u):
             c0, c1 = u * P, (u + 1) * P
-            nc.vector.quantize_mx(out=y_codes[h][:, c0:c1].bitcast(FP8X4), scales=y_scales[:, h * HALF + c0 : h * HALF + c1], in_=y_grouped[h][:, PACK * c0 : PACK * c1])
+            nc.vector.quantize_mx(out=y_codes[:, c0:c1].bitcast(FP8X4), scales=y_scales[:, c0:c1], in_=y_grouped[:, PACK * c0 : PACK * c1])
 
-        interleave(nc.vector, 0, 0)
-        interleave(nc.vector, 0, 1)
-        quantise_result(0, 0)
-        interleave(nc.vector, 1, 0)
-        interleave(nc.scalar, 1, 1)
-        quantise_result(0, 1)
-        quantise_result(1, 1)
-        quantise_result(1, 0)
+        interleave(nc.vector, 0, 128)
+        interleave(nc.scalar, 320, 512)
+        interleave(nc.vector, 128, 256)
+        quantise_result(0)
+        interleave(nc.vector, 256, 320)
+        quantise_result(1)
+        quantise_result(3)
+        quantise_result(2)
         for h in range(2):
-            nc.sync.dma_start(out_words[:, h * HALF : (h + 1) * HALF], y_codes[h][:].bitcast(I32))
-        for q in range(4):
-            queue = nc.scalar if q % 2 else nc.sync
-            queue.dma_start(out_2[0][4 * q : 4 * q + 4, :].bitcast(I32), y_scales[32 * q : 32 * q + 4, :].bitcast(I32))
+            cols = slice(h * HALF, (h + 1) * HALF)
+            nc.sync.dma_start(out_words[:, cols], y_codes[:, cols].bitcast(I32))
+        for r in range(4):
+            queue = nc.scalar if r % 2 else nc.sync
+            queue.dma_start(out_2[0][r:16:4, :].bitcast(I32), y_scales[r:P:32, :].bitcast(I32))

@@ -27,9 +27,9 @@ def tile_picked_phdiff_relu_po_kernel(tc, x_words, x_scales, w1, w2, offs, old, 
         stage = ctx.enter_context(tc.tile_pool(name="stage", bufs=1))
         psum = ctx.enter_context(tc.psum_pool(name="psum", bufs=1))
 
-        word_table = keep.tile([P, T], I32, align_bytes=64)
-        x_rows = x_words[0].rearrange("p c r -> p (c r)").bitcast(I32)
-        nc.sync.dma_start(word_table[:, : T // 8], x_rows[:, : T // 8])
+        w1_raw = keep.tile([P, PACK * N], F32)
+        w1_rows = w1.rearrange("(p j) c -> p (j c)", j=PACK)
+        nc.sync.dma_start(w1_raw[:, :256], w1_rows[:, :256])
         lists = []
         for name, src in (("offs", offs), ("old", old)):
             tile = keep.tile([P, S // 16], U16, name=name + "_list")
@@ -39,6 +39,7 @@ def tile_picked_phdiff_relu_po_kernel(tc, x_words, x_scales, w1, w2, offs, old, 
         scale_table = stage.tile([P, T], U8, offset=0)
         nc.vector.memset(scale_table[:].bitcast(I32), 0)
         nc.sync.dma_start(scale_table[0:P:8, :].bitcast(I32), x_scales[0].bitcast(I32))
+        nc.sync.dma_start(w1_raw[:, 256:], w1_rows[:, 256:])
         planes = [keep.tile([P, S], U8, name="plane%d" % i, align_bytes=64) for i in range(2)]
         for plane in planes:
             nc.vector.memset(plane[:].bitcast(I32), 0)
@@ -48,9 +49,8 @@ def tile_picked_phdiff_relu_po_kernel(tc, x_words, x_scales, w1, w2, offs, old, 
         warmed = keep.tile([P, 8], F32)
         nc.scalar.activation(warmed[:], warm[:], RELU)
 
-        w1_raw = keep.tile([P, PACK, N], F32)
-        nc.sync.dma_start(w1_raw[:], w1.rearrange("(p j) c -> p j c", j=PACK))
-        nc.sync.dma_start(word_table[:, T // 8 :], x_rows[:, T // 8 :])
+        word_table = keep.tile([P, T], I32, align_bytes=64)
+        nc.sync.dma_start(word_table[:], x_words[0].rearrange("p c r -> p (c r)").bitcast(I32))
 
         picked_scales = []
         for i in range(2):
@@ -63,8 +63,8 @@ def tile_picked_phdiff_relu_po_kernel(tc, x_words, x_scales, w1, w2, offs, old, 
                 nc.sync.dma_start(planes[i][r:P:32, :].bitcast(I32), picked_scales[i][8 * r : P : 32, :].bitcast(I32))
 
         place_scale_rows(0)
-        w2_raw = stage.tile([P, PACK, N], F32, offset=0)
-        nc.sync.dma_start(w2_raw[:], w2.rearrange("(p j) c -> p j c", j=PACK))
+        w2_raw = stage.tile([P, PACK * N], F32, offset=0)
+        nc.sync.dma_start(w2_raw[:], w2.rearrange("(p j) c -> p (j c)", j=PACK))
         place_scale_rows(1)
 
         def gather_words(words, offsets):
@@ -74,18 +74,18 @@ def tile_picked_phdiff_relu_po_kernel(tc, x_words, x_scales, w1, w2, offs, old, 
 
         def round_and_deal(engine, grouped, raw, u, m0, m1, sign):
             dst = grouped[:].rearrange("p (t m j) -> p m j t", t=PACK, j=PACK)[:, m0:m1, :, 2 * u : 2 * u + 2]
-            src = raw[:].rearrange("p j (m t) -> p m j t", t=PACK)[:, m0:m1, :, 2 * u : 2 * u + 2]
+            src = raw[:].rearrange("p (j m t) -> p m j t", j=PACK, t=PACK)[:, m0:m1, :, 2 * u : 2 * u + 2]
             if engine is nc.scalar:
                 nc.scalar.activation(dst, src, COPY, scale=sign)
             else:
                 nc.vector.tensor_scalar_mul(dst, src, sign)
 
-        def quantise(raw, name, sign, step):
+        def quantise(raw, name, sign, step, splits):
             grouped = keep.tile([P, PACK * N], BF16, name=name + "_grouped", align_bytes=64)
-            round_and_deal(nc.scalar, grouped, raw, 0, 0, 40, sign)
-            round_and_deal(nc.vector, grouped, raw, 0, 40, P, sign)
-            round_and_deal(nc.scalar, grouped, raw, 1, 0, 80, sign)
-            round_and_deal(nc.vector, grouped, raw, 1, 80, P, sign)
+            for u in range(2):
+                round_and_deal(nc.scalar, grouped, raw, u, 0, splits[u], sign)
+                if splits[u] < P:
+                    round_and_deal(nc.vector, grouped, raw, u, splits[u], P, sign)
             codes = keep.tile([P, N], U32, name=name + "_codes", align_bytes=64)
             scales = keep.tile([P, N], U8, name=name + "_scales", align_bytes=64)
             for t in range(0, PACK, step):
@@ -93,11 +93,10 @@ def tile_picked_phdiff_relu_po_kernel(tc, x_words, x_scales, w1, w2, offs, old, 
                 nc.vector.quantize_mx(out=codes[:, cols].bitcast(FP8X4), scales=scales[:, cols], in_=grouped[:, t * N : (t + step) * N])
             return codes, scales
 
-        w1_mx = quantise(w1_raw, "w1", 1.0, 2)
-        picked_words = [
-            [gather_words(keep.tile([P, HALF], U32, name="words%d_%d" % (i, h), align_bytes=64), lists[i][:, 16 * h : 16 * h + 16])[:] for h in range(2)]
-            for i in range(2)
-        ]
+        w1_mx = quantise(w1_raw, "w1", 1.0, 2, (64, 80))
+        now_words = [gather_words(keep.tile([P, HALF], U32, name="now_words%d" % h, align_bytes=64), lists[0][:, 16 * h : 16 * h + 16])[:] for h in range(2)]
+        old_words = gather_words(keep.tile([P, S], U32, name="old_words", align_bytes=64), lists[1][:])
+        picked_words = [now_words, [old_words[:, :HALF], old_words[:, HALF:]]]
 
         banks = [[psum.tile([P, HALF], F32, name="bank%d_%d" % (h, t)) for t in range(PACK)] for h in range(2)]
 
@@ -117,25 +116,24 @@ def tile_picked_phdiff_relu_po_kernel(tc, x_words, x_scales, w1, w2, offs, old, 
         for h in range(2):
             for t in range(PACK):
                 one_pass(0, w1_mx, h, t)
-        w2_mx = quantise(w2_raw, "w2", -1.0, 1)
-        for t in range(PACK):
-            for h in range(2):
-                one_pass(1, w2_mx, h, t)
+        w2_mx = quantise(w2_raw, "w2", -1.0, 1, (40, 80))
+        order = [(t, h) for u in range(2) for h in range(2) for t in (2 * u, 2 * u + 1)]
+        for t, h in order:
+            one_pass(1, w2_mx, h, t)
 
         out_rows = out_0.rearrange("(p t) j -> p t j", t=PACK)
         out_words = out_1[0].rearrange("p c r -> p (c r)").bitcast(I32)
         y_scales = keep.tile([P, S], U8, align_bytes=64)
         y = keep.tile([P, PACK, S], F32)
-        for t in range(PACK):
-            for h in range(2):
-                cols = slice(h * HALF, (h + 1) * HALF)
-                if (t, h) in ((1, 0), (1, 1), (2, 1)):
-                    nc.vector.tensor_scalar_max(y[:, t, cols], banks[h][t][:], 0.0)
-                else:
-                    nc.scalar.activation(y[:, t, cols], banks[h][t][:], RELU)
-                if t == 0:
-                    nc.sync.dma_start(out_rows[:, t, cols], y[:, t, cols])
-            if t == 1:
+        for t, h in order:
+            cols = slice(h * HALF, (h + 1) * HALF)
+            if (t, h) in ((0, 1), (3, 0), (2, 1)):
+                nc.vector.tensor_scalar_max(y[:, t, cols], banks[h][t][:], 0.0)
+            else:
+                nc.scalar.activation(y[:, t, cols], banks[h][t][:], RELU)
+            if t == 0:
+                nc.sync.dma_start(out_rows[:, t, cols], y[:, t, cols])
+            elif (t, h) == (1, 1):
                 nc.sync.dma_start(out_rows[:, t, :], y[:, t, :])
         nc.sync.dma_start(out_rows[:, 2:, :], y[:, 2:, :])
 
@@ -155,10 +153,10 @@ def tile_picked_phdiff_relu_po_kernel(tc, x_words, x_scales, w1, w2, offs, old, 
             nc.vector.quantize_mx(out=y_codes[:, c0:c1].bitcast(FP8X4), scales=y_scales[:, c0:c1], in_=y_grouped[:, PACK * c0 : PACK * c1])
 
         interleave(nc.vector, 0, 128)
-        interleave(nc.scalar, 320, 512)
+        interleave(nc.scalar, 352, 512)
         interleave(nc.vector, 128, 256)
         quantise_result(0)
-        interleave(nc.vector, 256, 320)
+        interleave(nc.vector, 256, 352)
         quantise_result(1)
         quantise_result(3)
         quantise_result(2)

@@ -18,6 +18,15 @@ RELU = mybir.ActivationFunctionType.Relu
 P = 128
 PACK = 4
 HALF = S // 2
+GROUP = 16
+QUADRANT = 32
+BLOCK = 8
+
+W1_HEAD = 256
+W1_SCALAR_COLUMNS = (64, 80)
+W2_SCALAR_COLUMNS = (40, 80)
+VECTOR_BANKS = ((0, 1), (3, 0), (2, 1))
+SCALAR_FROM = 384
 
 
 def tile_picked_phdiff_relu_po_kernel(tc, x_words, x_scales, w1, w2, offs, old, out_0, out_1, out_2):
@@ -29,17 +38,17 @@ def tile_picked_phdiff_relu_po_kernel(tc, x_words, x_scales, w1, w2, offs, old, 
 
         w1_raw = keep.tile([P, PACK * N], F32)
         w1_rows = w1.rearrange("(p j) c -> p (j c)", j=PACK)
-        nc.sync.dma_start(w1_raw[:, :256], w1_rows[:, :256])
+        nc.sync.dma_start(w1_raw[:, :W1_HEAD], w1_rows[:, :W1_HEAD])
         lists = []
         for name, src in (("offs", offs), ("old", old)):
-            tile = keep.tile([P, S // 16], U16, name=name + "_list")
+            tile = keep.tile([P, S // GROUP], U16, name=name + "_list")
             nc.sync.dma_start(tile[:], src)
             lists.append(tile)
 
         scale_table = stage.tile([P, T], U8, offset=0)
         nc.vector.memset(scale_table[:].bitcast(I32), 0)
-        nc.sync.dma_start(scale_table[0:P:8, :].bitcast(I32), x_scales[0].bitcast(I32))
-        nc.sync.dma_start(w1_raw[:, 256:], w1_rows[:, 256:])
+        nc.sync.dma_start(scale_table[0:P:BLOCK, :].bitcast(I32), x_scales[0].bitcast(I32))
+        nc.sync.dma_start(w1_raw[:, W1_HEAD:], w1_rows[:, W1_HEAD:])
         planes = [keep.tile([P, S], U8, name="plane%d" % i, align_bytes=64) for i in range(2)]
         for plane in planes:
             nc.vector.memset(plane[:].bitcast(I32), 0)
@@ -59,8 +68,8 @@ def tile_picked_phdiff_relu_po_kernel(tc, x_words, x_scales, w1, w2, offs, old, 
             picked_scales.append(picked)
 
         def place_scale_rows(i):
-            for r in range(4):
-                nc.sync.dma_start(planes[i][r:P:32, :].bitcast(I32), picked_scales[i][8 * r : P : 32, :].bitcast(I32))
+            for r in range(QUADRANT // BLOCK):
+                nc.sync.dma_start(planes[i][r:P:QUADRANT, :].bitcast(I32), picked_scales[i][BLOCK * r : P : QUADRANT, :].bitcast(I32))
 
         place_scale_rows(0)
         w2_raw = stage.tile([P, PACK * N], F32, offset=0)
@@ -71,30 +80,32 @@ def tile_picked_phdiff_relu_po_kernel(tc, x_words, x_scales, w1, w2, offs, old, 
             nc.vector.tensor_copy(words[:], word_table[:].bitcast(U32).indirect(offsets))
             return words
 
-
-        def round_and_deal(engine, grouped, raw, u, m0, m1, sign):
-            dst = grouped[:].rearrange("p (t m j) -> p m j t", t=PACK, j=PACK)[:, m0:m1, :, 2 * u : 2 * u + 2]
-            src = raw[:].rearrange("p (j m t) -> p m j t", j=PACK, t=PACK)[:, m0:m1, :, 2 * u : 2 * u + 2]
+        def round_and_deal(engine, grouped, raw, pair, m0, m1, sign):
+            dst = grouped[:].rearrange("p (t m j) -> p m j t", t=PACK, j=PACK)[:, m0:m1, :, 2 * pair : 2 * pair + 2]
+            src = raw[:].rearrange("p (j m t) -> p m j t", j=PACK, t=PACK)[:, m0:m1, :, 2 * pair : 2 * pair + 2]
             if engine is nc.scalar:
                 nc.scalar.activation(dst, src, COPY, scale=sign)
             else:
                 nc.vector.tensor_scalar_mul(dst, src, sign)
 
-        def quantise(raw, name, sign, step, splits):
+        def quantise_weight(raw, name, sign, products_a_call, scalar_columns):
             grouped = keep.tile([P, PACK * N], BF16, name=name + "_grouped", align_bytes=64)
-            for u in range(2):
-                round_and_deal(nc.scalar, grouped, raw, u, 0, splits[u], sign)
-                if splits[u] < P:
-                    round_and_deal(nc.vector, grouped, raw, u, splits[u], P, sign)
+            for pair in range(2):
+                round_and_deal(nc.scalar, grouped, raw, pair, 0, scalar_columns[pair], sign)
+                round_and_deal(nc.vector, grouped, raw, pair, scalar_columns[pair], P, sign)
             codes = keep.tile([P, N], U32, name=name + "_codes", align_bytes=64)
             scales = keep.tile([P, N], U8, name=name + "_scales", align_bytes=64)
-            for t in range(0, PACK, step):
-                cols = slice(t * P, (t + step) * P)
-                nc.vector.quantize_mx(out=codes[:, cols].bitcast(FP8X4), scales=scales[:, cols], in_=grouped[:, t * N : (t + step) * N])
+            for t in range(0, PACK, products_a_call):
+                cols = slice(t * P, (t + products_a_call) * P)
+                nc.vector.quantize_mx(out=codes[:, cols].bitcast(FP8X4), scales=scales[:, cols], in_=grouped[:, t * N : (t + products_a_call) * N])
             return codes, scales
 
-        w1_mx = quantise(w1_raw, "w1", 1.0, 2, (64, 80))
-        now_words = [gather_words(keep.tile([P, HALF], U32, name="now_words%d" % h, align_bytes=64), lists[0][:, 16 * h : 16 * h + 16])[:] for h in range(2)]
+        w1_mx = quantise_weight(w1_raw, "w1", 1.0, 2, W1_SCALAR_COLUMNS)
+        list_half = HALF // GROUP
+        now_words = [
+            gather_words(keep.tile([P, HALF], U32, name="now_words%d" % h, align_bytes=64), lists[0][:, list_half * h : list_half * (h + 1)])[:]
+            for h in range(2)
+        ]
         old_words = gather_words(keep.tile([P, S], U32, name="old_words", align_bytes=64), lists[1][:])
         picked_words = [now_words, [old_words[:, :HALF], old_words[:, HALF:]]]
 
@@ -116,8 +127,9 @@ def tile_picked_phdiff_relu_po_kernel(tc, x_words, x_scales, w1, w2, offs, old, 
         for h in range(2):
             for t in range(PACK):
                 one_pass(0, w1_mx, h, t)
-        w2_mx = quantise(w2_raw, "w2", -1.0, 1, (40, 80))
-        order = [(t, h) for u in range(2) for h in range(2) for t in (2 * u, 2 * u + 1)]
+
+        w2_mx = quantise_weight(w2_raw, "w2", -1.0, 1, W2_SCALAR_COLUMNS)
+        order = [(t, h) for pair in range(2) for h in range(2) for t in (2 * pair, 2 * pair + 1)]
         for t, h in order:
             one_pass(1, w2_mx, h, t)
 
@@ -127,7 +139,7 @@ def tile_picked_phdiff_relu_po_kernel(tc, x_words, x_scales, w1, w2, offs, old, 
         y = keep.tile([P, PACK, S], F32)
         for t, h in order:
             cols = slice(h * HALF, (h + 1) * HALF)
-            if (t, h) in ((0, 1), (3, 0), (2, 1)):
+            if (t, h) in VECTOR_BANKS:
                 nc.vector.tensor_scalar_max(y[:, t, cols], banks[h][t][:], 0.0)
             else:
                 nc.scalar.activation(y[:, t, cols], banks[h][t][:], RELU)
@@ -148,21 +160,21 @@ def tile_picked_phdiff_relu_po_kernel(tc, x_words, x_scales, w1, w2, offs, old, 
             else:
                 nc.vector.tensor_copy(dst, src)
 
-        def quantise_result(u):
-            c0, c1 = u * P, (u + 1) * P
+        def quantise_result(quarter):
+            c0, c1 = quarter * P, (quarter + 1) * P
             nc.vector.quantize_mx(out=y_codes[:, c0:c1].bitcast(FP8X4), scales=y_scales[:, c0:c1], in_=y_grouped[:, PACK * c0 : PACK * c1])
 
-        interleave(nc.vector, 0, 128)
-        interleave(nc.scalar, 352, 512)
-        interleave(nc.vector, 128, 256)
+        interleave(nc.vector, 0, P)
+        interleave(nc.scalar, SCALAR_FROM, S)
+        interleave(nc.vector, P, HALF)
         quantise_result(0)
-        interleave(nc.vector, 256, 352)
+        interleave(nc.vector, HALF, SCALAR_FROM)
         quantise_result(1)
         quantise_result(3)
         quantise_result(2)
         for h in range(2):
             cols = slice(h * HALF, (h + 1) * HALF)
             nc.sync.dma_start(out_words[:, cols], y_codes[:, cols].bitcast(I32))
-        for r in range(4):
+        for r in range(QUADRANT // BLOCK):
             queue = nc.scalar if r % 2 else nc.sync
-            queue.dma_start(out_2[0][r:16:4, :].bitcast(I32), y_scales[r:P:32, :].bitcast(I32))
+            queue.dma_start(out_2[0][r : P // BLOCK : QUADRANT // BLOCK, :].bitcast(I32), y_scales[r:P:QUADRANT, :].bitcast(I32))

@@ -22,9 +22,9 @@ GROUP = 16
 QUADRANT = 32
 BLOCK = 8
 
-W1_HEAD = 256
-W1_SCALAR_COLUMNS = (64, 80)
-W2_SCALAR_COLUMNS = (40, 80)
+WORD_HEAD = 256
+W1_SCALAR = (64, 96)
+W2_SCALAR = (40, 80)
 VECTOR_BANKS = ((0, 1), (3, 0), (2, 1))
 SCALAR_FROM = 384
 
@@ -33,116 +33,114 @@ def tile_picked_phdiff_relu_po_kernel(tc, x_words, x_scales, w1, w2, offs, old, 
     nc = tc.nc
     with ExitStack() as ctx:
         keep = ctx.enter_context(tc.tile_pool(name="keep", bufs=1))
-        stage = ctx.enter_context(tc.tile_pool(name="stage", bufs=1))
+        shared = ctx.enter_context(tc.tile_pool(name="shared", bufs=1))
+        reused = ctx.enter_context(tc.tile_pool(name="reused", bufs=1))
         psum = ctx.enter_context(tc.psum_pool(name="psum", bufs=1))
 
-        w1_raw = keep.tile([P, PACK * N], F32)
-        w1_rows = w1.rearrange("(p j) c -> p (j c)", j=PACK)
-        nc.sync.dma_start(w1_raw[:, :W1_HEAD], w1_rows[:, :W1_HEAD])
-        lists = []
-        for name, src in (("offs", offs), ("old", old)):
-            tile = keep.tile([P, S // GROUP], U16, name=name + "_list")
-            nc.sync.dma_start(tile[:], src)
-            lists.append(tile)
-
-        scale_table = stage.tile([P, T], U8, offset=0)
+        word_table = keep.tile([P, T], I32, align_bytes=64)
+        word_rows = x_words[0].rearrange("p c r -> p (c r)").bitcast(I32)
+        nc.sync.dma_start(word_table[:, :WORD_HEAD], word_rows[:, :WORD_HEAD])
+        now_list = keep.tile([P, S // GROUP], U16)
+        nc.sync.dma_start(now_list[:], offs)
+        old_list = keep.tile([P, S // GROUP], U16)
+        nc.sync.dma_start(old_list[:], old)
+        scale_table = shared.tile([P, T], U8, offset=0)
         nc.vector.memset(scale_table[:].bitcast(I32), 0)
         nc.sync.dma_start(scale_table[0:P:BLOCK, :].bitcast(I32), x_scales[0].bitcast(I32))
-        nc.sync.dma_start(w1_raw[:, W1_HEAD:], w1_rows[:, W1_HEAD:])
-        planes = [keep.tile([P, S], U8, name="plane%d" % i, align_bytes=64) for i in range(2)]
-        for plane in planes:
-            nc.vector.memset(plane[:].bitcast(I32), 0)
+        nc.sync.dma_start(word_table[:, WORD_HEAD:], word_rows[:, WORD_HEAD:])
+        w1_raw = keep.tile([P, PACK * N], F32)
+        nc.sync.dma_start(w1_raw[:], w1.rearrange("(p j) c -> p (j c)", j=PACK))
 
         warm = keep.tile([P, 8], F32)
         nc.vector.memset(warm[:], 0.0)
         warmed = keep.tile([P, 8], F32)
         nc.scalar.activation(warmed[:], warm[:], RELU)
 
-        word_table = keep.tile([P, T], I32, align_bytes=64)
-        nc.sync.dma_start(word_table[:], x_words[0].rearrange("p c r -> p (c r)").bitcast(I32))
+        def plane_of(name, offsets):
+            plane = keep.tile([P, S], U8, name=name + "_plane", align_bytes=64)
+            nc.vector.memset(plane[:].bitcast(I32), 0)
+            picked = keep.tile([P, S], U8, name=name + "_picked", align_bytes=64)
+            nc.vector.tensor_copy(picked[:], scale_table[:].indirect(offsets))
+            return plane, picked
 
-        picked_scales = []
-        for i in range(2):
-            picked = keep.tile([P, S], U8, name="picked%d" % i, align_bytes=64)
-            nc.vector.tensor_copy(picked[:], scale_table[:].indirect(lists[i][:]))
-            picked_scales.append(picked)
-
-        def place_scale_rows(i):
+        def place(plane, picked):
             for r in range(QUADRANT // BLOCK):
-                nc.sync.dma_start(planes[i][r:P:QUADRANT, :].bitcast(I32), picked_scales[i][BLOCK * r : P : QUADRANT, :].bitcast(I32))
+                nc.sync.dma_start(plane[r:P:QUADRANT, :].bitcast(I32), picked[BLOCK * r : P : QUADRANT, :].bitcast(I32))
 
-        place_scale_rows(0)
-        w2_raw = stage.tile([P, PACK * N], F32, offset=0)
+        now_plane, now_picked = plane_of("now", now_list[:])
+        old_plane, old_picked = plane_of("old", old_list[:])
+        place(now_plane, now_picked)
+        w2_raw = shared.tile([P, PACK * N], F32, offset=0)
         nc.sync.dma_start(w2_raw[:], w2.rearrange("(p j) c -> p (j c)", j=PACK))
-        place_scale_rows(1)
+        place(old_plane, old_picked)
 
         def gather_words(words, offsets):
             nc.vector.tensor_copy(words[:], word_table[:].bitcast(U32).indirect(offsets))
-            return words
 
-        def round_and_deal(engine, grouped, raw, pair, m0, m1, sign):
-            dst = grouped[:].rearrange("p (t m j) -> p m j t", t=PACK, j=PACK)[:, m0:m1, :, 2 * pair : 2 * pair + 2]
-            src = raw[:].rearrange("p (j m t) -> p m j t", j=PACK, t=PACK)[:, m0:m1, :, 2 * pair : 2 * pair + 2]
-            if engine is nc.scalar:
-                nc.scalar.activation(dst, src, COPY, scale=sign)
-            else:
-                nc.vector.tensor_scalar_mul(dst, src, sign)
-
-        def quantise_weight(raw, name, sign, products_a_call, scalar_columns):
-            grouped = keep.tile([P, PACK * N], BF16, name=name + "_grouped", align_bytes=64)
-            for pair in range(2):
-                round_and_deal(nc.scalar, grouped, raw, pair, 0, scalar_columns[pair], sign)
-                round_and_deal(nc.vector, grouped, raw, pair, scalar_columns[pair], P, sign)
-            codes = keep.tile([P, N], U32, name=name + "_codes", align_bytes=64)
-            scales = keep.tile([P, N], U8, name=name + "_scales", align_bytes=64)
-            for t in range(0, PACK, products_a_call):
-                cols = slice(t * P, (t + products_a_call) * P)
-                nc.vector.quantize_mx(out=codes[:, cols].bitcast(FP8X4), scales=scales[:, cols], in_=grouped[:, t * N : (t + products_a_call) * N])
-            return codes, scales
-
-        w1_mx = quantise_weight(w1_raw, "w1", 1.0, 2, W1_SCALAR_COLUMNS)
         list_half = HALF // GROUP
-        now_words = [
-            gather_words(keep.tile([P, HALF], U32, name="now_words%d" % h, align_bytes=64), lists[0][:, list_half * h : list_half * (h + 1)])[:]
-            for h in range(2)
-        ]
-        old_words = gather_words(keep.tile([P, S], U32, name="old_words", align_bytes=64), lists[1][:])
-        picked_words = [now_words, [old_words[:, :HALF], old_words[:, HALF:]]]
+        now_words = keep.tile([P, S], U32, align_bytes=64)
+        gather_words(now_words, now_list[:])
+        old_first = keep.tile([P, HALF], U32, align_bytes=64)
+        gather_words(old_first, old_list[:, :list_half])
 
-        banks = [[psum.tile([P, HALF], F32, name="bank%d_%d" % (h, t)) for t in range(PACK)] for h in range(2)]
+        def round_pair(grouped, raw, pair, split, sign):
+            dst = grouped[:].rearrange("p (t m j) -> p m j t", t=2, j=PACK)
+            src = raw[:].rearrange("p (j m t) -> p m j t", j=PACK, t=PACK)[:, :, :, 2 * pair : 2 * pair + 2]
+            nc.scalar.activation(dst[:, :split], src[:, :split], COPY, scale=sign)
+            nc.vector.tensor_scalar_mul(dst[:, split:], src[:, split:], sign)
 
-        def one_pass(i, w_mx, h, t):
-            codes, scales = w_mx
+        def quantise(codes, scales, grouped, c0, c1, first):
+            nc.vector.quantize_mx(out=codes[:, c0:c1].bitcast(FP8X4), scales=scales[:, c0:c1], in_=grouped[:, PACK * (c0 - first) : PACK * (c1 - first)])
+
+        w1_pairs = [reused.tile([P, 2 * N], BF16, name="w1_pair%d" % pair, offset=pair * 4 * N, align_bytes=64) for pair in range(2)]
+        w1_codes = keep.tile([P, N], U32, align_bytes=64)
+        w1_scales = keep.tile([P, N], U8, align_bytes=64)
+        for pair in range(2):
+            round_pair(w1_pairs[pair], w1_raw, pair, W1_SCALAR[pair], 1.0)
+        quantise(w1_codes, w1_scales, w1_pairs[0], 0, P, 0)
+        quantise(w1_codes, w1_scales, w1_pairs[0], P, HALF, 0)
+        old_second = reused.tile([P, HALF], U32, offset=0, align_bytes=64)
+        gather_words(old_second, old_list[:, list_half:])
+        quantise(w1_codes, w1_scales, w1_pairs[1], HALF, N, HALF)
+
+        moving = [[now_words[:, :HALF], now_words[:, HALF:]], [old_first[:], old_second[:]]]
+        planes = [now_plane, old_plane]
+        order = [(t, h) for pair in range(2) for h in range(2) for t in (2 * pair, 2 * pair + 1)]
+        banks = {(t, h): psum.tile([P, HALF], F32, name="bank%d_%d" % (t, h)) for t, h in order}
+
+        def one_pass(i, codes, scales, t, h):
             cols = slice(t * P, (t + 1) * P)
             nc.tensor.matmul_mx(
-                out=banks[h][t][:],
+                out=banks[t, h][:],
                 lhsT=codes[:, cols].bitcast(FP8X4),
                 lhsT_scale=scales[:, cols],
-                rhs=picked_words[i][h].bitcast(FP8X4),
+                rhs=moving[i][h].bitcast(FP8X4),
                 rhs_scale=planes[i][:, h * HALF : (h + 1) * HALF],
                 start=(i == 0),
                 stop=(i == 1),
             )
 
-        for h in range(2):
-            for t in range(PACK):
-                one_pass(0, w1_mx, h, t)
-
-        w2_mx = quantise_weight(w2_raw, "w2", -1.0, 1, W2_SCALAR_COLUMNS)
-        order = [(t, h) for pair in range(2) for h in range(2) for t in (2 * pair, 2 * pair + 1)]
         for t, h in order:
-            one_pass(1, w2_mx, h, t)
+            one_pass(0, w1_codes, w1_scales, t, h)
+
+        w2_pairs = [keep.tile([P, 2 * N], BF16, name="w2_pair%d" % pair, align_bytes=64) for pair in range(2)]
+        w2_codes = keep.tile([P, N], U32, align_bytes=64)
+        w2_scales = keep.tile([P, N], U8, align_bytes=64)
+        for pair in range(2):
+            round_pair(w2_pairs[pair], w2_raw, pair, W2_SCALAR[pair], -1.0)
+        for t in range(PACK):
+            quantise(w2_codes, w2_scales, w2_pairs[t // 2], t * P, (t + 1) * P, t // 2 * HALF)
+        for t, h in order:
+            one_pass(1, w2_codes, w2_scales, t, h)
 
         out_rows = out_0.rearrange("(p t) j -> p t j", t=PACK)
-        out_words = out_1[0].rearrange("p c r -> p (c r)").bitcast(I32)
-        y_scales = keep.tile([P, S], U8, align_bytes=64)
         y = keep.tile([P, PACK, S], F32)
         for t, h in order:
             cols = slice(h * HALF, (h + 1) * HALF)
             if (t, h) in VECTOR_BANKS:
-                nc.vector.tensor_scalar_max(y[:, t, cols], banks[h][t][:], 0.0)
+                nc.vector.tensor_scalar_max(y[:, t, cols], banks[t, h][:], 0.0)
             else:
-                nc.scalar.activation(y[:, t, cols], banks[h][t][:], RELU)
+                nc.scalar.activation(y[:, t, cols], banks[t, h][:], RELU)
             if t == 0:
                 nc.sync.dma_start(out_rows[:, t, cols], y[:, t, cols])
             elif (t, h) == (1, 1):
@@ -151,6 +149,7 @@ def tile_picked_phdiff_relu_po_kernel(tc, x_words, x_scales, w1, w2, offs, old, 
 
         y_grouped = keep.tile([P, S * PACK], BF16, align_bytes=64)
         y_codes = keep.tile([P, S], U32, align_bytes=64)
+        y_scales = keep.tile([P, S], U8, align_bytes=64)
 
         def interleave(engine, c0, c1):
             dst = y_grouped[:].rearrange("p (c i t) -> p c t i", i=4, t=PACK)[:, c0 // 4 : c1 // 4]
@@ -160,18 +159,14 @@ def tile_picked_phdiff_relu_po_kernel(tc, x_words, x_scales, w1, w2, offs, old, 
             else:
                 nc.vector.tensor_copy(dst, src)
 
-        def quantise_result(quarter):
-            c0, c1 = quarter * P, (quarter + 1) * P
-            nc.vector.quantize_mx(out=y_codes[:, c0:c1].bitcast(FP8X4), scales=y_scales[:, c0:c1], in_=y_grouped[:, PACK * c0 : PACK * c1])
-
         interleave(nc.vector, 0, P)
         interleave(nc.scalar, SCALAR_FROM, S)
         interleave(nc.vector, P, HALF)
-        quantise_result(0)
+        quantise(y_codes, y_scales, y_grouped, 0, P, 0)
         interleave(nc.vector, HALF, SCALAR_FROM)
-        quantise_result(1)
-        quantise_result(3)
-        quantise_result(2)
+        for quarter in (1, 3, 2):
+            quantise(y_codes, y_scales, y_grouped, quarter * P, (quarter + 1) * P, 0)
+        out_words = out_1[0].rearrange("p c r -> p (c r)").bitcast(I32)
         for h in range(2):
             cols = slice(h * HALF, (h + 1) * HALF)
             nc.sync.dma_start(out_words[:, cols], y_codes[:, cols].bitcast(I32))

@@ -23,7 +23,7 @@ QUADRANT = 32
 BLOCK = 8
 
 WORD_HEAD = 256
-W1_SCALAR = (64, 96)
+W1_SCALAR = (48, 96)
 W2_SCALAR = (40, 80)
 VECTOR_BANKS = ((0, 1), (3, 0), (2, 1))
 SCALAR_FROM = 384
@@ -106,7 +106,7 @@ def tile_picked_phdiff_relu_po_kernel(tc, x_words, x_scales, w1, w2, offs, old, 
         moving = [[now_words[:, :HALF], now_words[:, HALF:]], [old_first[:], old_second[:]]]
         planes = [now_plane, old_plane]
         order = [(t, h) for pair in range(2) for h in range(2) for t in (2 * pair, 2 * pair + 1)]
-        banks = {(t, h): psum.tile([P, HALF], F32, name="bank%d_%d" % (t, h)) for t, h in order}
+        warm_bank = psum.tile([P, S], F32, offset=2048 * 7)
 
         def one_pass(i, codes, scales, t, h):
             cols = slice(t * P, (t + 1) * P)
@@ -120,6 +120,16 @@ def tile_picked_phdiff_relu_po_kernel(tc, x_words, x_scales, w1, w2, offs, old, 
                 stop=(i == 1),
             )
 
+        nc.tensor.matmul_mx(
+            out=warm_bank[:],
+            lhsT=now_words[:, :P].bitcast(FP8X4),
+            lhsT_scale=now_plane[:, :P],
+            rhs=now_words[:].bitcast(FP8X4),
+            rhs_scale=now_plane[:],
+            start=True,
+            stop=True,
+        )
+        banks = {(t, h): psum.tile([P, HALF], F32, name="bank%d_%d" % (t, h), offset=2048 * (2 * t + h)) for t, h in order}
         for t, h in order:
             one_pass(0, w1_codes, w1_scales, t, h)
 

@@ -24,9 +24,8 @@ BLOCK = 8
 
 WORD_HEAD = 256
 W1_SCALAR = (48, 96)
-W2_SCALAR = (40, 80)
+W2_SCALAR = (44, 60)
 VECTOR_BANKS = ((0, 1), (3, 0), (2, 1))
-SCALAR_FROM = 384
 
 
 def tile_picked_phdiff_relu_po_kernel(tc, x_words, x_scales, w1, w2, offs, old, out_0, out_1, out_2):
@@ -170,15 +169,15 @@ def tile_picked_phdiff_relu_po_kernel(tc, x_words, x_scales, w1, w2, offs, old, 
                 nc.vector.tensor_copy(dst, src)
 
         interleave(nc.vector, 0, P)
-        interleave(nc.scalar, SCALAR_FROM, S)
+        interleave(nc.scalar, HALF, 384)
         interleave(nc.vector, P, HALF)
         quantise(y_codes, y_scales, y_grouped, 0, P, 0)
-        interleave(nc.vector, HALF, SCALAR_FROM)
-        for quarter in (1, 3, 2):
+        interleave(nc.scalar, 384, 448)
+        interleave(nc.vector, 448, S)
+        for quarter in (1, 2, 3):
             quantise(y_codes, y_scales, y_grouped, quarter * P, (quarter + 1) * P, 0)
         out_words = out_1[0].rearrange("p c r -> p (c r)").bitcast(I32)
-        for h in range(2):
-            cols = slice(h * HALF, (h + 1) * HALF)
+        for cols in (slice(0, 384), slice(384, S)):
             nc.sync.dma_start(out_words[:, cols], y_codes[:, cols].bitcast(I32))
         for r in range(QUADRANT // BLOCK):
             queue = nc.scalar if r % 2 else nc.sync

@@ -24,8 +24,9 @@ BLOCK = 8
 
 WORD_HEAD = 256
 W1_SCALAR = (48, 96)
-W2_SCALAR = (44, 60)
-VECTOR_BANKS = ((0, 1), (3, 0), (2, 1))
+W2_SCALAR = (40, 64)
+W2_FILL = 92
+VECTOR_BANKS = ((1, 1), (3, 0), (2, 1))
 
 
 def tile_picked_phdiff_relu_po_kernel(tc, x_words, x_scales, w1, w2, offs, old, out_0, out_1, out_2):
@@ -82,11 +83,13 @@ def tile_picked_phdiff_relu_po_kernel(tc, x_words, x_scales, w1, w2, offs, old, 
         old_first = keep.tile([P, HALF], U32, align_bytes=64)
         gather_words(old_first, old_list[:, :list_half])
 
-        def round_pair(grouped, raw, pair, split, sign):
-            dst = grouped[:].rearrange("p (t m j) -> p m j t", t=2, j=PACK)
-            src = raw[:].rearrange("p (j m t) -> p m j t", j=PACK, t=PACK)[:, :, :, 2 * pair : 2 * pair + 2]
-            nc.scalar.activation(dst[:, :split], src[:, :split], COPY, scale=sign)
-            nc.vector.tensor_scalar_mul(dst[:, split:], src[:, split:], sign)
+        def round_columns(engine, grouped, raw, pair, m0, m1, sign):
+            dst = grouped[:].rearrange("p (t m j) -> p m j t", t=2, j=PACK)[:, m0:m1]
+            src = raw[:].rearrange("p (j m t) -> p m j t", j=PACK, t=PACK)[:, m0:m1, :, 2 * pair : 2 * pair + 2]
+            if engine is nc.scalar:
+                nc.scalar.activation(dst, src, COPY, scale=sign)
+            else:
+                nc.vector.tensor_scalar_mul(dst, src, sign)
 
         def quantise(codes, scales, grouped, c0, c1, first):
             nc.vector.quantize_mx(out=codes[:, c0:c1].bitcast(FP8X4), scales=scales[:, c0:c1], in_=grouped[:, PACK * (c0 - first) : PACK * (c1 - first)])
@@ -95,7 +98,8 @@ def tile_picked_phdiff_relu_po_kernel(tc, x_words, x_scales, w1, w2, offs, old, 
         w1_codes = keep.tile([P, N], U32, align_bytes=64)
         w1_scales = keep.tile([P, N], U8, align_bytes=64)
         for pair in range(2):
-            round_pair(w1_pairs[pair], w1_raw, pair, W1_SCALAR[pair], 1.0)
+            round_columns(nc.scalar, w1_pairs[pair], w1_raw, pair, 0, W1_SCALAR[pair], 1.0)
+            round_columns(nc.vector, w1_pairs[pair], w1_raw, pair, W1_SCALAR[pair], P, 1.0)
         quantise(w1_codes, w1_scales, w1_pairs[0], 0, P, 0)
         quantise(w1_codes, w1_scales, w1_pairs[0], P, HALF, 0)
         old_second = reused.tile([P, HALF], U32, offset=0, align_bytes=64)
@@ -136,9 +140,14 @@ def tile_picked_phdiff_relu_po_kernel(tc, x_words, x_scales, w1, w2, offs, old, 
         w2_codes = keep.tile([P, N], U32, align_bytes=64)
         w2_scales = keep.tile([P, N], U8, align_bytes=64)
         for pair in range(2):
-            round_pair(w2_pairs[pair], w2_raw, pair, W2_SCALAR[pair], -1.0)
-        for t in range(PACK):
+            round_columns(nc.scalar, w2_pairs[pair], w2_raw, pair, 0, W2_SCALAR[pair], -1.0)
+        round_columns(nc.vector, w2_pairs[0], w2_raw, 0, W2_SCALAR[0], P, -1.0)
+        round_columns(nc.vector, w2_pairs[1], w2_raw, 1, W2_SCALAR[1], W2_FILL, -1.0)
+        quantise(w2_codes, w2_scales, w2_pairs[0], 0, P, 0)
+        round_columns(nc.vector, w2_pairs[1], w2_raw, 1, W2_FILL, P, -1.0)
+        for t in range(1, PACK):
             quantise(w2_codes, w2_scales, w2_pairs[t // 2], t * P, (t + 1) * P, t // 2 * HALF)
+        order = [(0, 0), (0, 1), (1, 0), (1, 1), (2, 0), (3, 0), (2, 1), (3, 1)]
         for t, h in order:
             one_pass(1, w2_codes, w2_scales, t, h)
 

@@ -23,6 +23,7 @@ QUADRANT = 32
 BLOCK = 8
 
 WORD_HEAD = 256
+WARM = (256, 128)
 W1_SCALAR = (48, 96)
 W2_SCALAR = (40, 64)
 W2_FILL = 92
@@ -70,7 +71,7 @@ def tile_picked_phdiff_relu_po_kernel(tc, x_words, x_scales, w1, w2, offs, old, 
         now_plane, now_picked = plane_of("now", now_list[:])
         old_plane, old_picked = plane_of("old", old_list[:])
         place(now_plane, now_picked)
-        w2_raw = shared.tile([P, PACK * N], F32, offset=0)
+        w2_raw = keep.tile([P, PACK * N], F32)
         nc.sync.dma_start(w2_raw[:], w2.rearrange("(p j) c -> p (j c)", j=PACK))
         place(old_plane, old_picked)
 
@@ -123,15 +124,16 @@ def tile_picked_phdiff_relu_po_kernel(tc, x_words, x_scales, w1, w2, offs, old, 
                 stop=(i == 1),
             )
 
-        nc.tensor.matmul_mx(
-            out=warm_bank[:],
-            lhsT=now_words[:, :P].bitcast(FP8X4),
-            lhsT_scale=now_plane[:, :P],
-            rhs=now_words[:].bitcast(FP8X4),
-            rhs_scale=now_plane[:],
-            start=True,
-            stop=True,
-        )
+        for width in WARM:
+            nc.tensor.matmul_mx(
+                out=warm_bank[:, :width],
+                lhsT=now_words[:, :P].bitcast(FP8X4),
+                lhsT_scale=now_plane[:, :P],
+                rhs=now_words[:, :width].bitcast(FP8X4),
+                rhs_scale=now_plane[:, :width],
+                start=True,
+                stop=True,
+            )
         banks = {(t, h): psum.tile([P, HALF], F32, name="bank%d_%d" % (t, h), offset=2048 * (2 * t + h)) for t, h in order}
         for t, h in order:
             one_pass(0, w1_codes, w1_scales, t, h)

@@ -23,7 +23,6 @@ QUADRANT = 32
 BLOCK = 8
 
 WORD_HEAD = 256
-WARM = (256, 128)
 W1_SCALAR = (48, 96)
 W2_SCALAR = (40, 64)
 W2_FILL = 92
@@ -110,7 +109,6 @@ def tile_picked_phdiff_relu_po_kernel(tc, x_words, x_scales, w1, w2, offs, old, 
         moving = [[now_words[:, :HALF], now_words[:, HALF:]], [old_first[:], old_second[:]]]
         planes = [now_plane, old_plane]
         order = [(t, h) for pair in range(2) for h in range(2) for t in (2 * pair, 2 * pair + 1)]
-        warm_bank = psum.tile([P, S], F32, offset=2048 * 7)
 
         def one_pass(i, codes, scales, t, h):
             cols = slice(t * P, (t + 1) * P)
@@ -124,16 +122,6 @@ def tile_picked_phdiff_relu_po_kernel(tc, x_words, x_scales, w1, w2, offs, old, 
                 stop=(i == 1),
             )
 
-        for width in WARM:
-            nc.tensor.matmul_mx(
-                out=warm_bank[:, :width],
-                lhsT=now_words[:, :P].bitcast(FP8X4),
-                lhsT_scale=now_plane[:, :P],
-                rhs=now_words[:, :width].bitcast(FP8X4),
-                rhs_scale=now_plane[:, :width],
-                start=True,
-                stop=True,
-            )
         banks = {(t, h): psum.tile([P, HALF], F32, name="bank%d_%d" % (t, h), offset=2048 * (2 * t + h)) for t, h in order}
         for t, h in order:
             one_pass(0, w1_codes, w1_scales, t, h)

from contextlib import ExitStack

import concourse.mybir as mybir

K, T, S, N = 512, 2048, 512, 512
FLOPS = 2 * 2 * K * N * S

F32 = mybir.dt.float32
BF16 = mybir.dt.bfloat16
I32 = mybir.dt.int32
U32 = mybir.dt.uint32
U16 = mybir.dt.uint16
U8 = mybir.dt.uint8
FP8X4 = mybir.dt.float8_e4m3fn_x4
COPY = mybir.ActivationFunctionType.Copy
RELU = mybir.ActivationFunctionType.Relu

P = 128
PACK = 4
HALF = S // 2
GROUP = 16
QUADRANT = 32
BLOCK = 8

WORD_HEAD = 256
W1_SCALAR = (48, 96)
W2_SCALAR = (40, 64)
W2_FILL = 92
VECTOR_BANKS = ((1, 1), (3, 0), (2, 1))


def tile_picked_phdiff_relu_po_kernel(tc, x_words, x_scales, w1, w2, offs, old, out_0, out_1, out_2):
    nc = tc.nc
    with ExitStack() as ctx:
        keep = ctx.enter_context(tc.tile_pool(name="keep", bufs=1))
        shared = ctx.enter_context(tc.tile_pool(name="shared", bufs=1))
        reused = ctx.enter_context(tc.tile_pool(name="reused", bufs=1))
        psum = ctx.enter_context(tc.psum_pool(name="psum", bufs=1))

        word_table = keep.tile([P, T], I32, align_bytes=64)
        word_rows = x_words[0].rearrange("p c r -> p (c r)").bitcast(I32)
        nc.sync.dma_start(word_table[:, :WORD_HEAD], word_rows[:, :WORD_HEAD])
        now_list = keep.tile([P, S // GROUP], U16)
        nc.sync.dma_start(now_list[:], offs)
        old_list = keep.tile([P, S // GROUP], U16)
        nc.sync.dma_start(old_list[:], old)
        scale_table = shared.tile([P, T], U8, offset=0)
        nc.vector.memset(scale_table[:].bitcast(I32), 0)
        nc.sync.dma_start(scale_table[0:P:BLOCK, :].bitcast(I32), x_scales[0].bitcast(I32))
        nc.sync.dma_start(word_table[:, WORD_HEAD:], word_rows[:, WORD_HEAD:])
        w1_raw = keep.tile([P, PACK * N], F32)
        nc.sync.dma_start(w1_raw[:], w1.rearrange("(p j) c -> p (j c)", j=PACK))

        warm = keep.tile([P, 8], F32)
        nc.vector.memset(warm[:], 0.0)
        warmed = keep.tile([P, 8], F32)
        nc.scalar.activation(warmed[:], warm[:], RELU)

        def plane_of(name, offsets):
            plane = keep.tile([P, S], U8, name=name + "_plane", align_bytes=64)
            nc.vector.memset(plane[:].bitcast(I32), 0)
            picked = keep.tile([P, S], U8, name=name + "_picked", align_bytes=64)
            nc.vector.tensor_copy(picked[:], scale_table[:].indirect(offsets))
            return plane, picked

        def place(plane, picked):
            for r in range(QUADRANT // BLOCK):
                nc.sync.dma_start(plane[r:P:QUADRANT, :].bitcast(I32), picked[BLOCK * r : P : QUADRANT, :].bitcast(I32))

        now_plane, now_picked = plane_of("now", now_list[:])
        old_plane, old_picked = plane_of("old", old_list[:])
        place(now_plane, now_picked)
        w2_raw = keep.tile([P, PACK * N], F32)
        nc.sync.dma_start(w2_raw[:], w2.rearrange("(p j) c -> p (j c)", j=PACK))
        place(old_plane, old_picked)

        def gather_words(words, offsets):
            nc.vector.tensor_copy(words[:], word_table[:].bitcast(U32).indirect(offsets))

        list_half = HALF // GROUP
        now_words = keep.tile([P, S], U32, align_bytes=64)
        gather_words(now_words, now_list[:])
        old_first = keep.tile([P, HALF], U32, align_bytes=64)
        gather_words(old_first, old_list[:, :list_half])

        def round_columns(engine, grouped, raw, pair, m0, m1, sign):
            dst = grouped[:].rearrange("p (t m j) -> p m j t", t=2, j=PACK)[:, m0:m1]
            src = raw[:].rearrange("p (j m t) -> p m j t", j=PACK, t=PACK)[:, m0:m1, :, 2 * pair : 2 * pair + 2]
            if engine is nc.scalar:
                nc.scalar.activation(dst, src, COPY, scale=sign)
            else:
                nc.vector.tensor_scalar_mul(dst, src, sign)

        def quantise(codes, scales, grouped, c0, c1, first):
            nc.vector.quantize_mx(out=codes[:, c0:c1].bitcast(FP8X4), scales=scales[:, c0:c1], in_=grouped[:, PACK * (c0 - first) : PACK * (c1 - first)])

        w1_pairs = [reused.tile([P, 2 * N], BF16, name="w1_pair%d" % pair, offset=pair * 4 * N, align_bytes=64) for pair in range(2)]
        w1_codes = keep.tile([P, N], U32, align_bytes=64)
        w1_scales = keep.tile([P, N], U8, align_bytes=64)
        for pair in range(2):
            round_columns(nc.scalar, w1_pairs[pair], w1_raw, pair, 0, W1_SCALAR[pair], 1.0)
            round_columns(nc.vector, w1_pairs[pair], w1_raw, pair, W1_SCALAR[pair], P, 1.0)
        quantise(w1_codes, w1_scales, w1_pairs[0], 0, P, 0)
        quantise(w1_codes, w1_scales, w1_pairs[0], P, HALF, 0)
        old_second = reused.tile([P, HALF], U32, offset=0, align_bytes=64)
        gather_words(old_second, old_list[:, list_half:])
        quantise(w1_codes, w1_scales, w1_pairs[1], HALF, N, HALF)

        moving = [[now_words[:, :HALF], now_words[:, HALF:]], [old_first[:], old_second[:]]]
        planes = [now_plane, old_plane]
        order = [(t, h) for pair in range(2) for h in range(2) for t in (2 * pair, 2 * pair + 1)]

        def one_pass(i, codes, scales, t, h):
            cols = slice(t * P, (t + 1) * P)
            nc.tensor.matmul_mx(
                out=banks[t, h][:],
                lhsT=codes[:, cols].bitcast(FP8X4),
                lhsT_scale=scales[:, cols],
                rhs=moving[i][h].bitcast(FP8X4),
                rhs_scale=planes[i][:, h * HALF : (h + 1) * HALF],
                start=(i == 0),
                stop=(i == 1),
            )

        banks = {(t, h): psum.tile([P, HALF], F32, name="bank%d_%d" % (t, h), offset=2048 * (2 * t + h)) for t, h in order}
        for t, h in order:
            one_pass(0, w1_codes, w1_scales, t, h)

        w2_pairs = [keep.tile([P, 2 * N], BF16, name="w2_pair%d" % pair, align_bytes=64) for pair in range(2)]
        w2_codes = keep.tile([P, N], U32, align_bytes=64)
        w2_scales = keep.tile([P, N], U8, align_bytes=64)
        for pair in range(2):
            round_columns(nc.scalar, w2_pairs[pair], w2_raw, pair, 0, W2_SCALAR[pair], -1.0)
        round_columns(nc.vector, w2_pairs[0], w2_raw, 0, W2_SCALAR[0], P, -1.0)
        round_columns(nc.vector, w2_pairs[1], w2_raw, 1, W2_SCALAR[1], W2_FILL, -1.0)
        quantise(w2_codes, w2_scales, w2_pairs[0], 0, P, 0)
        round_columns(nc.vector, w2_pairs[1], w2_raw, 1, W2_FILL, P, -1.0)
        for t in range(1, PACK):
            quantise(w2_codes, w2_scales, w2_pairs[t // 2], t * P, (t + 1) * P, t // 2 * HALF)
        order = [(0, 0), (0, 1), (1, 0), (1, 1), (2, 0), (3, 0), (2, 1), (3, 1)]
        for t, h in order:
            one_pass(1, w2_codes, w2_scales, t, h)

        out_rows = out_0.rearrange("(p t) j -> p t j", t=PACK)
        y = keep.tile([P, PACK, S], F32)
        for t, h in order:
            cols = slice(h * HALF, (h + 1) * HALF)
            if (t, h) in VECTOR_BANKS:
                nc.vector.tensor_scalar_max(y[:, t, cols], banks[t, h][:], 0.0)
            else:
                nc.scalar.activation(y[:, t, cols], banks[t, h][:], RELU)
            if t == 0:
                nc.sync.dma_start(out_rows[:, t, cols], y[:, t, cols])
            elif (t, h) == (1, 1):
                nc.sync.dma_start(out_rows[:, t, :], y[:, t, :])
        nc.sync.dma_start(out_rows[:, 2:, :], y[:, 2:, :])

        y_grouped = keep.tile([P, S * PACK], BF16, align_bytes=64)
        y_codes = keep.tile([P, S], U32, align_bytes=64)
        y_scales = keep.tile([P, S], U8, align_bytes=64)

        def interleave(engine, c0, c1):
            dst = y_grouped[:].rearrange("p (c i t) -> p c t i", i=4, t=PACK)[:, c0 // 4 : c1 // 4]
            src = y[:].rearrange("p t (c i) -> p c t i", i=4)[:, c0 // 4 : c1 // 4]
            if engine is nc.scalar:
                nc.scalar.copy(dst, src)
            else:
                nc.vector.tensor_copy(dst, src)

        interleave(nc.vector, 0, P)
        interleave(nc.scalar, HALF, 384)
        interleave(nc.vector, P, HALF)
        quantise(y_codes, y_scales, y_grouped, 0, P, 0)
        interleave(nc.scalar, 384, 448)
        interleave(nc.vector, 448, S)
        for quarter in (1, 2, 3):
            quantise(y_codes, y_scales, y_grouped, quarter * P, (quarter + 1) * P, 0)
        out_words = out_1[0].rearrange("p c r -> p (c r)").bitcast(I32)
        for cols in (slice(0, 384), slice(384, S)):
            nc.sync.dma_start(out_words[:, cols], y_codes[:, cols].bitcast(I32))
        for r in range(QUADRANT // BLOCK):
            queue = nc.scalar if r % 2 else nc.sync
            queue.dma_start(out_2[0][r : P // BLOCK : QUADRANT // BLOCK, :].bitcast(I32), y_scales[r:P:QUADRANT, :].bitcast(I32))
